import numpy as np
import ml_dtypes


def mxq(x, axis, fmt="e4m3"):
    dtype, down = {"e4m3": (ml_dtypes.float8_e4m3fn, 7), "e5m2": (ml_dtypes.float8_e5m2, 14)}[fmt]
    v = np.moveaxis(np.asarray(x, np.float32).astype(ml_dtypes.bfloat16).astype(np.float64), axis, -1)
    blocks = v.reshape(v.shape[:-1] + (-1, 32))
    amax = np.abs(blocks).max(-1, keepdims=True)
    byte = np.maximum(np.where(amax > 0, np.frexp(amax)[1] - 1 + 127, 0) - down, 1)
    scale = np.exp2(byte - 127.0)
    codes = (blocks / scale).astype(np.float32).astype(dtype).astype(np.float64)
    return np.moveaxis((codes * scale).reshape(v.shape), -1, axis)


WIDE = False


def mx_kscale(k):
    if not WIDE:
        return np.ones(k)
    levels = np.array([10, -10, 5, -5, 0])
    if k % 512:
        return np.exp2(np.random.permutation(np.resize(levels, k // 32))).repeat(32)
    a = np.empty((k // 512, 16))
    for p in range(k // 512):
        a[p, :8] = np.random.permutation(np.resize(levels, 8))
        for g in range(8):
            far = levels[np.abs(levels - a[p, g]) >= 10]
            a[p, g + 8] = far[np.random.randint(len(far))]
    return np.exp2(a.ravel()).repeat(32)


def f64(x):
    return np.asarray(x).astype(np.float64)


def striped(idx):
    return np.tile(np.asarray(idx).reshape(-1, 16).T, (8, 1)).astype(np.uint16)


def unstriped(offs):
    return offs[:16].T.reshape(-1).astype(np.int64)


E2M1 = np.array([0.0, 0.5, 1.0, 1.5, 2.0, 3.0, 4.0, 6.0, -0.0, -0.5, -1.0, -1.5, -2.0, -3.0, -4.0, -6.0])


def pack_weight(w, fmt):
    k, n = w.shape
    w = f64(np.asarray(w, np.float32).astype(ml_dtypes.bfloat16)).reshape(k // 32, 32, n)
    amax = np.abs(w).max(1)
    if fmt == "e4m3":
        byte = np.frexp(amax)[1] - 1 + 127 - 7
    else:
        mant, ex = np.frexp(amax / 6.0)
        byte = np.where(mant > 0.5, ex, ex - 1) + 127
    byte = np.clip(np.where(amax > 0, byte, 1), 1, 254)
    scaled = (w * np.exp2(127.0 - byte)[:, None, :]).reshape(k, n).astype(np.float32)
    by_word = np.ascontiguousarray(scaled.reshape(k // 512, 128, 4, n).transpose(0, 1, 3, 2))
    if fmt == "e4m3":
        words = by_word.astype(ml_dtypes.float8_e4m3fn).view(np.uint8)
    else:
        c = by_word.astype(ml_dtypes.float4_e2m1fn).view(np.uint8) & 0xF
        words = (c[..., 0::2] | (c[..., 1::2] << 4)).reshape(k // 512, 128, 2 * n)
    return np.ascontiguousarray(words), np.ascontiguousarray(byte.astype(np.uint8).reshape(k // 512, 16, n))


def unpack_weight(words, scales, fmt):
    g, _, n = scales.shape
    words = np.ascontiguousarray(words).reshape(g, 128, n, -1)
    if fmt == "e4m3":
        vals = words.view(ml_dtypes.float8_e4m3fn).astype(np.float64)
    else:
        nib = np.empty((g, 128, n, 4), np.uint8)
        nib[..., 0::2] = words & 0xF
        nib[..., 1::2] = words >> 4
        vals = E2M1[nib]
    vals = vals * np.repeat(np.exp2(scales.astype(np.float64) - 127.0), 8, axis=1)[..., None]
    return vals.transpose(0, 1, 3, 2).reshape(g * 512, n)


def sigmoid(v):
    return 1.0 / (1.0 + np.exp(-v))


K, T, I, G, F, M = 512, 2048, 1024, 64, 512, 128


def setup_inputs():
    n = np.random.standard_normal
    idx = np.random.permutation(T)[:I]
    fk = mx_kscale(K)
    ff = mx_kscale(F)
    instp = pack_weight(n((K, T)) / fk[:, None], "e4m3")
    return {
        "inst_words": instp[0],
        "inst_scales": instp[1],
        "wv": (n((K, F)) * 1 / np.sqrt(K) * fk[:, None]).astype(np.float32),
        "wu": (n((K, F)) * 1 / np.sqrt(K) * fk[:, None]).astype(np.float32),
        "gain": (np.random.uniform(0.5, 2.0, (F, 1)) * ff[:, None]).astype(np.float32),
        "score": (n((F, M)) * 1 / np.sqrt(F) / ff[:, None]).astype(np.float32),
        "offs": striped(idx),
    }


def reference(inst_words, inst_scales, wv, wu, gain, score, offs):
    idx = unstriped(offs)
    instu = unpack_weight(inst_words, inst_scales, "e4m3")
    wvq = mxq(f64(wv), 0, "e4m3")
    instidxg = instu[:, idx]
    z = wvq.T @ instidxg
    wuq = mxq(f64(wu), 0, "e4m3")
    v = wuq.T @ instidxg
    x = np.tanh(z) * sigmoid(v) * f64(gain)
    scoreq = mxq(f64(score), 0, "e4m3")
    xq = mxq(x, 0, "e4m3")
    a = scoreq.T @ xq
    p = np.exp(a)
    s = p.reshape(M, G, I // G).sum(axis=2)
    sr = np.repeat(s, I // G, axis=1)
    y = p / sr * 16.0
    return y

@@ -1,0 +1,207 @@
+from contextlib import ExitStack
+
+import concourse.mybir as mybir
+
+F32 = mybir.dt.float32
+BF16 = mybir.dt.bfloat16
+I32 = mybir.dt.int32
+U32 = mybir.dt.uint32
+U16 = mybir.dt.uint16
+U8 = mybir.dt.uint8
+FP8X4 = mybir.dt.float8_e4m3fn_x4
+ALU = mybir.AluOpType
+ACT = mybir.ActivationFunctionType
+AXIS_X = mybir.AxisListType.X
+
+P = 128
+PACK = 4
+K, T, SLOTS, F, M = 512, 2048, 1024, 512, 128
+BAG = 16
+BANK = 512
+CHUNKS = (256, 512, 256)
+PIECE = 256
+GATE_LEAD = 5
+VECTOR_INTERLEAVES = 2
+PROJ_BANKS = 4
+
+FLOPS = 2 * (2 * K * F * SLOTS + F * M * SLOTS)
+
+
+def tile_attend_milweights_kernel(tc, inst_words, inst_scales, wv, wu, gain, score, offs, out):
+    nc = tc.nc
+    with ExitStack() as ctx:
+        keep = ctx.enter_context(tc.tile_pool(name="keep", bufs=1))
+        work = ctx.enter_context(tc.tile_pool(name="work", bufs=1))
+        psum = ctx.enter_context(tc.psum_pool(name="psum", bufs=1))
+
+        offsets = keep.tile([P, SLOTS // 16], U16, name="offsets")
+        pool_scales = keep.tile([P, T], U8, name="pool_scales", align_bytes=64)
+        pool_words = keep.tile([P, T], U32, name="pool_words", align_bytes=64)
+        gains = keep.tile([P, PACK], F32, name="gains")
+        wu_raw = keep.tile([P, PACK, F], F32, name="wu_raw")
+        wv_raw = keep.tile([P, PACK, F], F32, name="wv_raw")
+        score_raw = keep.tile([P, PACK, M], F32, name="score_raw")
+
+        wu_rows = wu.rearrange("(p j) f -> p j f", j=PACK)
+        nc.scalar.dma_start(out=wu_raw[:, :2, :], in_=wu_rows[:, :2, :])
+        nc.vector.memset(pool_scales[:].bitcast(I32), 0)
+        nc.sync.dma_start(offsets[:], offs)
+        nc.sync.dma_start(out=gains[:], in_=gain.rearrange("(p t) o -> p (t o)", t=PACK))
+        for r in range(4):
+            nc.sync.dma_start(
+                out=pool_scales[r:P:32, :].bitcast(I32), in_=inst_scales[0, r:16:4, :].bitcast(I32)
+            )
+        nc.sync.dma_start(out=wu_raw[:, 2:, :], in_=wu_rows[:, 2:, :])
+        nc.sync.dma_start(
+            out=pool_words[:].bitcast(I32),
+            in_=inst_words[0].rearrange("p n t -> p (n t)").bitcast(I32),
+        )
+        nc.sync.dma_start(out=wv_raw[:], in_=wv.rearrange("(p j) f -> p j f", j=PACK))
+        nc.sync.dma_start(out=score_raw[:], in_=score.rearrange("(p j) m -> p j m", j=PACK))
+
+        inst_s = keep.tile([P, SLOTS], U8, name="inst_s", align_bytes=64)
+        inst_w = keep.tile([P, SLOTS], U32, name="inst_w", align_bytes=64)
+        nc.vector.tensor_copy(inst_s[:], pool_scales[:].indirect(offsets[:]))
+
+        def quantise_projection(raw, name):
+            dealt = keep.tile([P, PACK, P, PACK], BF16, name=name + "_dealt", align_bytes=64)
+            codes = keep.tile([P, F], U32, name=name + "_codes", align_bytes=64)
+            scales = keep.tile([P, F], U8, name=name + "_scales", align_bytes=64)
+            src = raw[:].rearrange("p j (m t) -> p m j t", t=PACK)
+            dst = dealt[:].rearrange("p t m j -> p m j t")
+            nc.vector.tensor_copy(out=dst, in_=src)
+            flat = dealt[:].rearrange("p t m j -> p (t m j)")
+            for half in range(2):
+                cols = slice(half * 2 * P, (half + 1) * 2 * P)
+                nc.vector.quantize_mx(
+                    out=codes[:, cols].bitcast(FP8X4),
+                    scales=scales[:, cols],
+                    in_=flat[:, half * 2 * P * PACK : (half + 1) * 2 * P * PACK],
+                )
+            return codes, scales
+
+        starts = [sum(CHUNKS[:c]) for c in range(len(CHUNKS))]
+
+        ring = [psum.tile([P, BANK], F32, name="proj%d" % b) for b in range(PROJ_BANKS)]
+
+        def activate(weights, func, c, first, result, whole_bank):
+            codes, scales = weights
+            width = CHUNKS[c]
+            slots = slice(starts[c], starts[c] + width)
+            per_bank = BANK // width
+            bank = whole_bank[:].rearrange("p (u i) -> p u i", u=per_bank)
+            for u in range(per_bank):
+                cols = slice((first + u) * P, (first + u + 1) * P)
+                nc.tensor.matmul_mx(
+                    out=bank[:, u, :],
+                    lhsT=codes[:, cols].bitcast(FP8X4),
+                    lhsT_scale=scales[:, cols],
+                    rhs=inst_w[:, slots].bitcast(FP8X4),
+                    rhs_scale=inst_s[:, slots],
+                    start=True,
+                    stop=True,
+                )
+            nc.scalar.activation(out=result[:, first : first + per_bank, :], in_=bank, func=func)
+
+        wu_mx = quantise_projection(wu_raw, "wu")
+        for start, width in zip(starts, CHUNKS):
+            slots = slice(start, start + width)
+            cols = slice(start // 16, (start + width) // 16)
+            nc.vector.tensor_copy(inst_w[:, slots], pool_words[:].indirect(offsets[:, cols]))
+        wv_mx = quantise_projection(wv_raw, "wv")
+
+        score_packed = keep.tile([P, M, PACK], BF16, name="score_packed", align_bytes=64)
+        score_codes = keep.tile([P, M], U32, name="score_codes", align_bytes=64)
+        score_scales = keep.tile([P, M], U8, name="score_scales", align_bytes=64)
+        nc.vector.tensor_copy(
+            out=score_packed[:].rearrange("p (c i) j -> p c j i", i=4),
+            in_=score_raw[:].rearrange("p j (c i) -> p c j i", i=4),
+        )
+        nc.vector.quantize_mx(
+            out=score_codes[:].bitcast(FP8X4),
+            scales=score_scales[:],
+            in_=score_packed[:].rearrange("p m j -> p (m j)"),
+        )
+
+        gates = [work.tile([P, PACK, w], F32, name="gate%d" % c) for c, w in enumerate(CHUNKS)]
+        values = [work.tile([P, PACK, w], F32, name="value%d" % c) for c, w in enumerate(CHUNKS)]
+        parts = [(c, first) for c, width in enumerate(CHUNKS) for first in range(0, PACK, BANK // width)]
+        gate_steps = [(wu_mx, ACT.Sigmoid, c, first, gates[c]) for c, first in parts]
+        value_steps = [(wv_mx, ACT.Tanh, c, first, values[c]) for c, first in parts]
+        steps = gate_steps[:GATE_LEAD]
+        for n, value_step in enumerate(value_steps):
+            if n >= GATE_LEAD:
+                steps.append(gate_steps[n])
+            steps.append(value_step)
+        for n, step in enumerate(steps):
+            activate(*step, ring[n % PROJ_BANKS])
+
+        shifted = []
+        for c, width in enumerate(CHUNKS):
+            bags = width // BAG
+            x_rows = work.tile([P, PACK, width], BF16, name="x_rows%d" % c)
+            for t in range(PACK):
+                nc.vector.scalar_tensor_tensor(
+                    out=x_rows[:, t, :],
+                    in0=gates[c][:, t, :],
+                    scalar=gains[:, t : t + 1],
+                    in1=values[c][:, t, :],
+                    op0=ALU.mult,
+                    op1=ALU.mult,
+                )
+            x_packed = work.tile([P, width, PACK], BF16, name="x_packed%d" % c, align_bytes=64)
+            for low in range(0, width, PIECE):
+                on_vector = (starts[c] + low) // PIECE < VECTOR_INTERLEAVES
+                interleave = nc.vector.tensor_copy if on_vector else nc.scalar.copy
+                interleave(
+                    out=x_packed[:, low : low + PIECE, :].rearrange("p (c i) t -> p c t i", i=4),
+                    in_=x_rows[:, :, low : low + PIECE].rearrange("p t (c i) -> p c t i", i=4),
+                )
+            x_codes = work.tile([P, width], U32, name="x_codes%d" % c, align_bytes=64)
+            x_scales = work.tile([P, width], U8, name="x_scales%d" % c, align_bytes=64)
+            nc.vector.quantize_mx(
+                out=x_codes[:].bitcast(FP8X4),
+                scales=x_scales[:],
+                in_=x_packed[:].rearrange("p i t -> p (i t)"),
+            )
+            logits = psum.tile([M, bags, BAG], F32, name="logits", bufs=len(CHUNKS))
+            nc.tensor.matmul_mx(
+                out=logits[:].rearrange("m g e -> m (g e)"),
+                lhsT=score_codes[:].bitcast(FP8X4),
+                lhsT_scale=score_scales[:],
+                rhs=x_codes[:].bitcast(FP8X4),
+                rhs_scale=x_scales[:],
+                start=True,
+                stop=True,
+            )
+            top = work.tile([M, bags], F32, name="top%d" % c)
+            nc.vector.tensor_reduce(out=top[:], in_=logits[:], axis=AXIS_X, op=ALU.max)
+            below = work.tile([M, bags, BAG], F32, name="below%d" % c)
+            nc.vector.tensor_tensor(
+                out=below[:],
+                in0=logits[:],
+                in1=top[:].unsqueeze(2).to_broadcast([M, bags, BAG]),
+                op=ALU.subtract,
+            )
+            shifted.append(below)
+
+        for c, width in enumerate(CHUNKS):
+            bags = width // BAG
+            p = work.tile([M, bags, BAG], F32, name="p%d" % c)
+            nc.scalar.activation(out=p[:], in_=shifted[c][:], func=ACT.Exp)
+            total = work.tile([M, bags], F32, name="total%d" % c)
+            nc.vector.tensor_reduce(out=total[:], in_=p[:], axis=AXIS_X, op=ALU.add)
+            inverse = work.tile([M, bags], F32, name="inverse%d" % c)
+            nc.vector.reciprocal(out=inverse[:], in_=total[:])
+            weights = work.tile([M, bags, BAG], F32, name="weights%d" % c)
+            nc.vector.scalar_tensor_tensor(
+                out=weights[:],
+                in0=p[:],
+                scalar=float(BAG),
+                in1=inverse[:].unsqueeze(2).to_broadcast([M, bags, BAG]),
+                op0=ALU.mult,
+                op1=ALU.mult,
+            )
+            nc.sync.dma_start(
+                out=out[:, starts[c] : starts[c] + width], in_=weights[:].rearrange("m g e -> m (g e)")
+            )

@@ -23,6 +23,7 @@ PIECE = 256
 GATE_LEAD = 5
 VECTOR_INTERLEAVES = 2
 PROJ_BANKS = 4
+WU_VECTOR_COLS = 64
 
 FLOPS = 2 * (2 * K * F * SLOTS + F * M * SLOTS)
 
@@ -42,11 +43,10 @@ def tile_attend_milweights_kernel(tc, inst_words, inst_scales, wv, wu, gain, sco
         wv_raw = keep.tile([P, PACK, F], F32, name="wv_raw")
         score_raw = keep.tile([P, PACK, M], F32, name="score_raw")
 
-        wu_rows = wu.rearrange("(p j) f -> p j f", j=PACK)
-        nc.scalar.dma_start(out=wu_raw[:, :2, :], in_=wu_rows[:, :2, :])
-        nc.vector.memset(pool_scales[:].bitcast(I32), 0)
         nc.sync.dma_start(offsets[:], offs)
-        nc.sync.dma_start(out=gains[:], in_=gain.rearrange("(p t) o -> p (t o)", t=PACK))
+        wu_rows = wu.rearrange("(p j) f -> p j f", j=PACK)
+        nc.sync.dma_start(out=wu_raw[:, :2, :], in_=wu_rows[:, :2, :])
+        nc.vector.memset(pool_scales[:].bitcast(I32), 0)
         for r in range(4):
             nc.sync.dma_start(
                 out=pool_scales[r:P:32, :].bitcast(I32), in_=inst_scales[0, r:16:4, :].bitcast(I32)
@@ -57,19 +57,26 @@ def tile_attend_milweights_kernel(tc, inst_words, inst_scales, wv, wu, gain, sco
             in_=inst_words[0].rearrange("p n t -> p (n t)").bitcast(I32),
         )
         nc.sync.dma_start(out=wv_raw[:], in_=wv.rearrange("(p j) f -> p j f", j=PACK))
+        nc.sync.dma_start(out=gains[:], in_=gain.rearrange("(p t) o -> p (t o)", t=PACK))
         nc.sync.dma_start(out=score_raw[:], in_=score.rearrange("(p j) m -> p j m", j=PACK))
 
-        inst_s = keep.tile([P, SLOTS], U8, name="inst_s", align_bytes=64)
+        warm = keep.tile([P, 1], F32, name="warm")
+        nc.gpsimd.memset(warm[:], 0.0)
+        nc.scalar.activation(out=warm[:], in_=warm[:], func=ACT.Sigmoid)
+        early = SLOTS - CHUNKS[-1]
+        early_scales = keep.tile([P, early], U8, name="early_scales", align_bytes=64)
         inst_w = keep.tile([P, SLOTS], U32, name="inst_w", align_bytes=64)
-        nc.vector.tensor_copy(inst_s[:], pool_scales[:].indirect(offsets[:]))
+        nc.vector.tensor_copy(early_scales[:], pool_scales[:].indirect(offsets[:, : early // 16]))
 
-        def quantise_projection(raw, name):
-            dealt = keep.tile([P, PACK, P, PACK], BF16, name=name + "_dealt", align_bytes=64)
+        def quantise_projection(raw, vector_cols, name):
+            dealt = keep.tile([P, PACK, P, PACK], BF16, name=name + "_dealt", tag=name + "_dealt", align_bytes=64)
             codes = keep.tile([P, F], U32, name=name + "_codes", align_bytes=64)
             scales = keep.tile([P, F], U8, name=name + "_scales", align_bytes=64)
             src = raw[:].rearrange("p j (m t) -> p m j t", t=PACK)
             dst = dealt[:].rearrange("p t m j -> p m j t")
-            nc.vector.tensor_copy(out=dst, in_=src)
+            if vector_cols < P:
+                nc.scalar.copy(out=dst[:, vector_cols:], in_=src[:, vector_cols:])
+            nc.vector.tensor_copy(out=dst[:, :vector_cols], in_=src[:, :vector_cols])
             flat = dealt[:].rearrange("p t m j -> p (t m j)")
             for half in range(2):
                 cols = slice(half * 2 * P, (half + 1) * 2 * P)
@@ -97,18 +104,22 @@ def tile_attend_milweights_kernel(tc, inst_words, inst_scales, wv, wu, gain, sco
                     lhsT=codes[:, cols].bitcast(FP8X4),
                     lhsT_scale=scales[:, cols],
                     rhs=inst_w[:, slots].bitcast(FP8X4),
-                    rhs_scale=inst_s[:, slots],
+                    rhs_scale=inst_scale_parts[c],
                     start=True,
                     stop=True,
                 )
             nc.scalar.activation(out=result[:, first : first + per_bank, :], in_=bank, func=func)
 
-        wu_mx = quantise_projection(wu_raw, "wu")
+        wu_mx = quantise_projection(wu_raw, WU_VECTOR_COLS, "wu")
         for start, width in zip(starts, CHUNKS):
             slots = slice(start, start + width)
             cols = slice(start // 16, (start + width) // 16)
             nc.vector.tensor_copy(inst_w[:, slots], pool_words[:].indirect(offsets[:, cols]))
-        wv_mx = quantise_projection(wv_raw, "wv")
+        wv_mx = quantise_projection(wv_raw, P, "wv")
+        late_scales = keep.tile([P, CHUNKS[-1]], U8, name="late_scales", tag="wv_dealt", align_bytes=64)
+        nc.vector.tensor_copy(late_scales[:], pool_scales[:].indirect(offsets[:, early // 16 :]))
+        inst_scale_parts = [early_scales[:, start : start + width] for start, width in zip(starts[:-1], CHUNKS)]
+        inst_scale_parts.append(late_scales[:])
 
         score_packed = keep.tile([P, M, PACK], BF16, name="score_packed", align_bytes=64)
         score_codes = keep.tile([P, M], U32, name="score_codes", align_bytes=64)
@@ -136,9 +147,8 @@ def tile_attend_milweights_kernel(tc, inst_words, inst_scales, wv, wu, gain, sco
         for n, step in enumerate(steps):
             activate(*step, ring[n % PROJ_BANKS])
 
-        shifted = []
-        for c, width in enumerate(CHUNKS):
-            bags = width // BAG
+        def score_chunk(c):
+            width = CHUNKS[c]
             x_rows = work.tile([P, PACK, width], BF16, name="x_rows%d" % c)
             for t in range(PACK):
                 nc.vector.scalar_tensor_tensor(
@@ -164,7 +174,7 @@ def tile_attend_milweights_kernel(tc, inst_words, inst_scales, wv, wu, gain, sco
                 scales=x_scales[:],
                 in_=x_packed[:].rearrange("p i t -> p (i t)"),
             )
-            logits = psum.tile([M, bags, BAG], F32, name="logits", bufs=len(CHUNKS))
+            logits = psum.tile([M, width // BAG, BAG], F32, name="logits%d" % c)
             nc.tensor.matmul_mx(
                 out=logits[:].rearrange("m g e -> m (g e)"),
                 lhsT=score_codes[:].bitcast(FP8X4),
@@ -174,6 +184,10 @@ def tile_attend_milweights_kernel(tc, inst_words, inst_scales, wv, wu, gain, sco
                 start=True,
                 stop=True,
             )
+            return logits
+
+        def shift(c, logits):
+            bags = CHUNKS[c] // BAG
             top = work.tile([M, bags], F32, name="top%d" % c)
             nc.vector.tensor_reduce(out=top[:], in_=logits[:], axis=AXIS_X, op=ALU.max)
             below = work.tile([M, bags, BAG], F32, name="below%d" % c)
@@ -183,12 +197,15 @@ def tile_attend_milweights_kernel(tc, inst_words, inst_scales, wv, wu, gain, sco
                 in1=top[:].unsqueeze(2).to_broadcast([M, bags, BAG]),
                 op=ALU.subtract,
             )
-            shifted.append(below)
+            return below
 
-        for c, width in enumerate(CHUNKS):
-            bags = width // BAG
-            p = work.tile([M, bags, BAG], F32, name="p%d" % c)
-            nc.scalar.activation(out=p[:], in_=shifted[c][:], func=ACT.Exp)
+        def exponentiate(c, below):
+            p = work.tile([M, CHUNKS[c] // BAG, BAG], F32, name="p%d" % c)
+            nc.scalar.activation(out=p[:], in_=below[:], func=ACT.Exp)
+            return p
+
+        def normalise(c, p):
+            bags = CHUNKS[c] // BAG
             total = work.tile([M, bags], F32, name="total%d" % c)
             nc.vector.tensor_reduce(out=total[:], in_=p[:], axis=AXIS_X, op=ALU.add)
             inverse = work.tile([M, bags], F32, name="inverse%d" % c)
@@ -203,5 +220,14 @@ def tile_attend_milweights_kernel(tc, inst_words, inst_scales, wv, wu, gain, sco
                 op1=ALU.mult,
             )
             nc.sync.dma_start(
-                out=out[:, starts[c] : starts[c] + width], in_=weights[:].rearrange("m g e -> m (g e)")
+                out=out[:, starts[c] : starts[c] + CHUNKS[c]], in_=weights[:].rearrange("m g e -> m (g e)")
             )
+
+        below_a = shift(0, score_chunk(0))
+        logits_b = score_chunk(1)
+        p_a = exponentiate(0, below_a)
+        logits_c = score_chunk(2)
+        p_b = exponentiate(1, shift(1, logits_b))
+        p_c = exponentiate(2, shift(2, logits_c))
+        for c, p in enumerate((p_a, p_b, p_c)):
+            normalise(c, p)

@@ -24,6 +24,7 @@ GATE_LEAD = 5
 VECTOR_INTERLEAVES = 2
 PROJ_BANKS = 4
 WU_VECTOR_COLS = 64
+SCALAR_PIECES = 2
 
 FLOPS = 2 * (2 * K * F * SLOTS + F * M * SLOTS)
 
@@ -149,7 +150,7 @@ def tile_attend_milweights_kernel(tc, inst_words, inst_scales, wv, wu, gain, sco
 
         def score_chunk(c):
             width = CHUNKS[c]
-            x_rows = work.tile([P, PACK, width], BF16, name="x_rows%d" % c)
+            x_rows = work.tile([P, PACK, width], BF16, name="x_rows%d" % c, tag="x_rows%d" % c)
             for t in range(PACK):
                 nc.vector.scalar_tensor_tensor(
                     out=x_rows[:, t, :],
@@ -199,8 +200,8 @@ def tile_attend_milweights_kernel(tc, inst_words, inst_scales, wv, wu, gain, sco
             )
             return below
 
-        def exponentiate(c, below):
-            p = work.tile([M, CHUNKS[c] // BAG, BAG], F32, name="p%d" % c)
+        def exponentiate(c, below, tag):
+            p = work.tile([M, CHUNKS[c] // BAG, BAG], F32, name="p%d" % c, tag=tag)
             nc.scalar.activation(out=p[:], in_=below[:], func=ACT.Exp)
             return p
 
@@ -211,23 +212,36 @@ def tile_attend_milweights_kernel(tc, inst_words, inst_scales, wv, wu, gain, sco
             inverse = work.tile([M, bags], F32, name="inverse%d" % c)
             nc.vector.reciprocal(out=inverse[:], in_=total[:])
             weights = work.tile([M, bags, BAG], F32, name="weights%d" % c)
-            nc.vector.scalar_tensor_tensor(
-                out=weights[:],
-                in0=p[:],
-                scalar=float(BAG),
-                in1=inverse[:].unsqueeze(2).to_broadcast([M, bags, BAG]),
-                op0=ALU.mult,
-                op1=ALU.mult,
-            )
-            nc.sync.dma_start(
-                out=out[:, starts[c] : starts[c] + CHUNKS[c]], in_=weights[:].rearrange("m g e -> m (g e)")
-            )
+            piece_bags = PIECE // BAG
+            for low in range(0, bags, piece_bags):
+                piece = slice(low, low + piece_bags)
+                first_slot = starts[c] + low * BAG
+                if first_slot // PIECE < SCALAR_PIECES:
+                    factor = work.tile([M, piece_bags], F32, name="factor%d" % c)
+                    nc.scalar.activation(out=factor[:], in_=inverse[:, piece], func=ACT.Copy, scale=float(BAG))
+                    for g in range(piece_bags):
+                        nc.scalar.activation(
+                            out=weights[:, low + g, :], in_=p[:, low + g, :], func=ACT.Copy, scale=factor[:, g : g + 1]
+                        )
+                else:
+                    nc.vector.scalar_tensor_tensor(
+                        out=weights[:, piece, :],
+                        in0=p[:, piece, :],
+                        scalar=float(BAG),
+                        in1=inverse[:, piece].unsqueeze(2).to_broadcast([M, piece_bags, BAG]),
+                        op0=ALU.mult,
+                        op1=ALU.mult,
+                    )
+                nc.sync.dma_start(
+                    out=out[:, first_slot : first_slot + PIECE],
+                    in_=weights[:, piece, :].rearrange("m g e -> m (g e)"),
+                )
 
         below_a = shift(0, score_chunk(0))
         logits_b = score_chunk(1)
-        p_a = exponentiate(0, below_a)
         logits_c = score_chunk(2)
-        p_b = exponentiate(1, shift(1, logits_b))
-        p_c = exponentiate(2, shift(2, logits_c))
+        p_a = exponentiate(0, below_a, "x_rows2")
+        p_b = exponentiate(1, shift(1, logits_b), "x_rows1")
+        p_c = exponentiate(2, shift(2, logits_c), "x_rows0")
         for c, p in enumerate((p_a, p_b, p_c)):
             normalise(c, p)

@@ -18,13 +18,14 @@ PACK = 4
 K, T, SLOTS, F, M = 512, 2048, 1024, 512, 128
 BAG = 16
 BANK = 512
-CHUNKS = (256, 512, 256)
-PIECE = 256
-GATE_LEAD = 5
-VECTOR_INTERLEAVES = 2
+QUARTER = 256
+PIECES = (256, 256, 256, 128, 128)
+GROUPS = ((0, 1), (2,), (3, 4))
 PROJ_BANKS = 4
-WU_VECTOR_COLS = 64
-SCALAR_PIECES = 2
+WU_VECTOR_COLS = 70
+WV_VECTOR_COLS = 92
+RUN = 4
+SCALAR_GATES = (3,)
 
 FLOPS = 2 * (2 * K * F * SLOTS + F * M * SLOTS)
 
@@ -33,7 +34,6 @@ def tile_attend_milweights_kernel(tc, inst_words, inst_scales, wv, wu, gain, sco
     nc = tc.nc
     with ExitStack() as ctx:
         keep = ctx.enter_context(tc.tile_pool(name="keep", bufs=1))
-        work = ctx.enter_context(tc.tile_pool(name="work", bufs=1))
         psum = ctx.enter_context(tc.psum_pool(name="psum", bufs=1))
 
         offsets = keep.tile([P, SLOTS // 16], U16, name="offsets")
@@ -41,7 +41,7 @@ def tile_attend_milweights_kernel(tc, inst_words, inst_scales, wv, wu, gain, sco
         pool_words = keep.tile([P, T], U32, name="pool_words", align_bytes=64)
         gains = keep.tile([P, PACK], F32, name="gains")
         wu_raw = keep.tile([P, PACK, F], F32, name="wu_raw")
-        wv_raw = keep.tile([P, PACK, F], F32, name="wv_raw")
+        wv_raw = keep.tile([P, PACK, F], F32, name="wv_raw", tag="wv_raw")
         score_raw = keep.tile([P, PACK, M], F32, name="score_raw")
 
         nc.sync.dma_start(offsets[:], offs)
@@ -63,11 +63,15 @@ def tile_attend_milweights_kernel(tc, inst_words, inst_scales, wv, wu, gain, sco
 
         warm = keep.tile([P, 1], F32, name="warm")
         nc.gpsimd.memset(warm[:], 0.0)
-        nc.scalar.activation(out=warm[:], in_=warm[:], func=ACT.Sigmoid)
-        early = SLOTS - CHUNKS[-1]
-        early_scales = keep.tile([P, early], U8, name="early_scales", align_bytes=64)
-        inst_w = keep.tile([P, SLOTS], U32, name="inst_w", align_bytes=64)
-        nc.vector.tensor_copy(early_scales[:], pool_scales[:].indirect(offsets[:, : early // 16]))
+        nc.scalar.activation(out=warm[:], in_=warm[:], func=ACT.Tanh)
+
+        half_gains = keep.tile([P, PACK], F32, name="half_gains")
+        nc.gpsimd.tensor_scalar(out=half_gains[:], in0=gains[:], scalar1=0.5, scalar2=None, op0=ALU.mult)
+
+        def gather(pool, dtype, low, high, name, tag):
+            picked = keep.tile([P, high - low], dtype, name=name, tag=tag, align_bytes=64)
+            nc.vector.tensor_copy(picked[:], pool[:].indirect(offsets[:, low // 16 : high // 16]))
+            return [picked[:, at : at + QUARTER] for at in range(0, high - low, QUARTER)]
 
         def quantise_projection(raw, vector_cols, name):
             dealt = keep.tile([P, PACK, P, PACK], BF16, name=name + "_dealt", tag=name + "_dealt", align_bytes=64)
@@ -75,109 +79,114 @@ def tile_attend_milweights_kernel(tc, inst_words, inst_scales, wv, wu, gain, sco
             scales = keep.tile([P, F], U8, name=name + "_scales", align_bytes=64)
             src = raw[:].rearrange("p j (m t) -> p m j t", t=PACK)
             dst = dealt[:].rearrange("p t m j -> p m j t")
-            if vector_cols < P:
-                nc.scalar.copy(out=dst[:, vector_cols:], in_=src[:, vector_cols:])
+            nc.scalar.copy(out=dst[:, vector_cols:], in_=src[:, vector_cols:])
             nc.vector.tensor_copy(out=dst[:, :vector_cols], in_=src[:, :vector_cols])
-            flat = dealt[:].rearrange("p t m j -> p (t m j)")
-            for half in range(2):
-                cols = slice(half * 2 * P, (half + 1) * 2 * P)
-                nc.vector.quantize_mx(
-                    out=codes[:, cols].bitcast(FP8X4),
-                    scales=scales[:, cols],
-                    in_=flat[:, half * 2 * P * PACK : (half + 1) * 2 * P * PACK],
-                )
+            nc.vector.quantize_mx(
+                out=codes[:].bitcast(FP8X4), scales=scales[:], in_=dealt[:].rearrange("p t m j -> p (t m j)")
+            )
             return codes, scales
 
-        starts = [sum(CHUNKS[:c]) for c in range(len(CHUNKS))]
-
         ring = [psum.tile([P, BANK], F32, name="proj%d" % b) for b in range(PROJ_BANKS)]
+        turn = [0]
 
-        def activate(weights, func, c, first, result, whole_bank):
+        def project(weights, scale, low, width, result):
             codes, scales = weights
-            width = CHUNKS[c]
-            slots = slice(starts[c], starts[c] + width)
+            quarter, at = divmod(low, QUARTER)
             per_bank = BANK // width
-            bank = whole_bank[:].rearrange("p (u i) -> p u i", u=per_bank)
-            for u in range(per_bank):
-                cols = slice((first + u) * P, (first + u + 1) * P)
-                nc.tensor.matmul_mx(
-                    out=bank[:, u, :],
-                    lhsT=codes[:, cols].bitcast(FP8X4),
-                    lhsT_scale=scales[:, cols],
-                    rhs=inst_w[:, slots].bitcast(FP8X4),
-                    rhs_scale=inst_scale_parts[c],
-                    start=True,
-                    stop=True,
-                )
-            nc.scalar.activation(out=result[:, first : first + per_bank, :], in_=bank, func=func)
+            for first in range(0, PACK, per_bank):
+                bank = ring[turn[0] % PROJ_BANKS][:].rearrange("p (u i) -> p u i", u=per_bank)
+                turn.append(turn.pop() + 1)
+                for u in range(per_bank):
+                    cols = slice((first + u) * P, (first + u + 1) * P)
+                    nc.tensor.matmul_mx(
+                        out=bank[:, u, :],
+                        lhsT=codes[:, cols].bitcast(FP8X4),
+                        lhsT_scale=scales[:, cols],
+                        rhs=inst_w[quarter][:, at : at + width].bitcast(FP8X4),
+                        rhs_scale=inst_s[quarter][:, at : at + width],
+                        start=True,
+                        stop=True,
+                    )
+                nc.scalar.activation(out=result[:, first : first + per_bank, :], in_=bank, func=ACT.Tanh, scale=scale)
 
+        def gate_tanh(q, tag, align):
+            result = keep.tile([P, PACK, QUARTER], F32, name="gate_tanh%d" % q, tag=tag, align_bytes=align)
+            project(wu_mx, 0.5, q * QUARTER, QUARTER, result)
+            return result
+
+        def gate(q, tanh_half, result):
+            for t in range(PACK):
+                factor = half_gains[:, t : t + 1]
+                if q in SCALAR_GATES:
+                    nc.scalar.activation(
+                        out=result[:, t, :], in_=tanh_half[:, t, :], func=ACT.Identity, scale=factor, bias=factor
+                    )
+                else:
+                    nc.vector.tensor_scalar(
+                        out=result[:, t, :],
+                        in0=tanh_half[:, t, :],
+                        scalar1=1.0,
+                        scalar2=factor,
+                        op0=ALU.add,
+                        op1=ALU.mult,
+                    )
+            return result
+
+        starts = [sum(PIECES[:c]) for c in range(len(PIECES))]
+
+        def value(c):
+            result = keep.tile([P, PACK, PIECES[c]], F32, name="value%d" % c)
+            project(wv_mx, 1.0, starts[c], PIECES[c], result)
+            return result
+
+        early = SLOTS - QUARTER
+        inst_s = gather(pool_scales, U8, 0, early, "early_scales", "early_scales")
         wu_mx = quantise_projection(wu_raw, WU_VECTOR_COLS, "wu")
-        for start, width in zip(starts, CHUNKS):
-            slots = slice(start, start + width)
-            cols = slice(start // 16, (start + width) // 16)
-            nc.vector.tensor_copy(inst_w[:, slots], pool_words[:].indirect(offsets[:, cols]))
-        wv_mx = quantise_projection(wv_raw, P, "wv")
-        late_scales = keep.tile([P, CHUNKS[-1]], U8, name="late_scales", tag="wv_dealt", align_bytes=64)
-        nc.vector.tensor_copy(late_scales[:], pool_scales[:].indirect(offsets[:, early // 16 :]))
-        inst_scale_parts = [early_scales[:, start : start + width] for start, width in zip(starts[:-1], CHUNKS)]
-        inst_scale_parts.append(late_scales[:])
+        inst_w = gather(pool_words, U32, 0, QUARTER, "first_words", "first_words")
+        inst_w.extend(gather(pool_words, U32, QUARTER, SLOTS, "later_words", "wu_dealt"))
+        tanh0 = gate_tanh(0, "gate_tanh0", 64)
+        wv_mx = quantise_projection(wv_raw, WV_VECTOR_COLS, "wv")
+        tanh1 = gate_tanh(1, "wv_raw", None)
+        after_wv = keep.tile([P, PACK * QUARTER + PACK * M // 2], F32, name="after_wv", tag="wv_dealt", align_bytes=64)
+        gate_tiles = [after_wv[:, : PACK * QUARTER].rearrange("p (t i) -> p t i", t=PACK)]
+        for q in range(1, SLOTS // QUARTER):
+            gate_tiles.append(keep.tile([P, PACK, QUARTER], F32, name="gate%d" % q)[:])
+        gates = [gate(0, tanh0, gate_tiles[0])]
+        inst_s.extend(gather(pool_scales, U8, early, SLOTS, "late_scales", "gate_tanh0"))
+        gates.append(gate(1, tanh1, gate_tiles[1]))
 
-        score_packed = keep.tile([P, M, PACK], BF16, name="score_packed", align_bytes=64)
+        score_packed = after_wv[:, PACK * QUARTER :].bitcast(BF16).rearrange("p (m j) -> p m j", j=PACK)
         score_codes = keep.tile([P, M], U32, name="score_codes", align_bytes=64)
         score_scales = keep.tile([P, M], U8, name="score_scales", align_bytes=64)
         nc.vector.tensor_copy(
-            out=score_packed[:].rearrange("p (c i) j -> p c j i", i=4),
+            out=score_packed.rearrange("p (c i) j -> p c j i", i=4),
             in_=score_raw[:].rearrange("p j (c i) -> p c j i", i=4),
         )
         nc.vector.quantize_mx(
             out=score_codes[:].bitcast(FP8X4),
             scales=score_scales[:],
-            in_=score_packed[:].rearrange("p m j -> p (m j)"),
+            in_=score_packed.rearrange("p m j -> p (m j)"),
         )
 
-        gates = [work.tile([P, PACK, w], F32, name="gate%d" % c) for c, w in enumerate(CHUNKS)]
-        values = [work.tile([P, PACK, w], F32, name="value%d" % c) for c, w in enumerate(CHUNKS)]
-        parts = [(c, first) for c, width in enumerate(CHUNKS) for first in range(0, PACK, BANK // width)]
-        gate_steps = [(wu_mx, ACT.Sigmoid, c, first, gates[c]) for c, first in parts]
-        value_steps = [(wv_mx, ACT.Tanh, c, first, values[c]) for c, first in parts]
-        steps = gate_steps[:GATE_LEAD]
-        for n, value_step in enumerate(value_steps):
-            if n >= GATE_LEAD:
-                steps.append(gate_steps[n])
-            steps.append(value_step)
-        for n, step in enumerate(steps):
-            activate(*step, ring[n % PROJ_BANKS])
-
-        def score_chunk(c):
-            width = CHUNKS[c]
-            x_rows = work.tile([P, PACK, width], BF16, name="x_rows%d" % c, tag="x_rows%d" % c)
-            for t in range(PACK):
-                nc.vector.scalar_tensor_tensor(
-                    out=x_rows[:, t, :],
-                    in0=gates[c][:, t, :],
-                    scalar=gains[:, t : t + 1],
-                    in1=values[c][:, t, :],
-                    op0=ALU.mult,
-                    op1=ALU.mult,
-                )
-            x_packed = work.tile([P, width, PACK], BF16, name="x_packed%d" % c, align_bytes=64)
-            for low in range(0, width, PIECE):
-                on_vector = (starts[c] + low) // PIECE < VECTOR_INTERLEAVES
-                interleave = nc.vector.tensor_copy if on_vector else nc.scalar.copy
-                interleave(
-                    out=x_packed[:, low : low + PIECE, :].rearrange("p (c i) t -> p c t i", i=4),
-                    in_=x_rows[:, :, low : low + PIECE].rearrange("p t (c i) -> p c t i", i=4),
-                )
-            x_codes = work.tile([P, width], U32, name="x_codes%d" % c, align_bytes=64)
-            x_scales = work.tile([P, width], U8, name="x_scales%d" % c, align_bytes=64)
+        def score_piece(c, logits):
+            width = PIECES[c]
+            quarter, at = divmod(starts[c], QUARTER)
+            x_packed = keep.tile([P, width, PACK], BF16, name="x_packed%d" % c, align_bytes=64)
+            nc.vector.tensor_tensor(
+                out=x_packed[:].rearrange("p (c i) t -> p c t i", i=RUN),
+                in0=gates[quarter][:, :, at : at + width].rearrange("p t (c i) -> p c t i", i=RUN),
+                in1=values[c][:].rearrange("p t (c i) -> p c t i", i=RUN),
+                op=ALU.mult,
+            )
+            x_codes = keep.tile([P, width], U32, name="x_codes%d" % c, align_bytes=64)
+            x_scales = keep.tile([P, width], U8, name="x_scales%d" % c, align_bytes=64)
             nc.vector.quantize_mx(
                 out=x_codes[:].bitcast(FP8X4),
                 scales=x_scales[:],
                 in_=x_packed[:].rearrange("p i t -> p (i t)"),
             )
-            logits = psum.tile([M, width // BAG, BAG], F32, name="logits%d" % c)
             nc.tensor.matmul_mx(
-                out=logits[:].rearrange("m g e -> m (g e)"),
+                out=logits,
                 lhsT=score_codes[:].bitcast(FP8X4),
                 lhsT_scale=score_scales[:],
                 rhs=x_codes[:].bitcast(FP8X4),
@@ -185,63 +194,51 @@ def tile_attend_milweights_kernel(tc, inst_words, inst_scales, wv, wu, gain, sco
                 start=True,
                 stop=True,
             )
-            return logits
 
-        def shift(c, logits):
-            bags = CHUNKS[c] // BAG
-            top = work.tile([M, bags], F32, name="top%d" % c)
-            nc.vector.tensor_reduce(out=top[:], in_=logits[:], axis=AXIS_X, op=ALU.max)
-            below = work.tile([M, bags, BAG], F32, name="below%d" % c)
+        def softmax(g, logits):
+            width = sum(PIECES[c] for c in GROUPS[g])
+            bags = width // BAG
+            by_bag = logits.rearrange("m (g e) -> m g e", e=BAG)
+            top = keep.tile([M, bags], F32, name="top%d" % g)
+            nc.vector.tensor_reduce(out=top[:], in_=by_bag, axis=AXIS_X, op=ALU.max)
+            below = keep.tile([M, bags, BAG], F32, name="below%d" % g)
             nc.vector.tensor_tensor(
-                out=below[:],
-                in0=logits[:],
-                in1=top[:].unsqueeze(2).to_broadcast([M, bags, BAG]),
-                op=ALU.subtract,
+                out=below[:], in0=by_bag, in1=top[:].unsqueeze(2).to_broadcast([M, bags, BAG]), op=ALU.subtract
             )
-            return below
-
-        def exponentiate(c, below, tag):
-            p = work.tile([M, CHUNKS[c] // BAG, BAG], F32, name="p%d" % c, tag=tag)
+            p = keep.tile([M, bags, BAG], F32, name="p%d" % g)
             nc.scalar.activation(out=p[:], in_=below[:], func=ACT.Exp)
-            return p
-
-        def normalise(c, p):
-            bags = CHUNKS[c] // BAG
-            total = work.tile([M, bags], F32, name="total%d" % c)
+            total = keep.tile([M, bags], F32, name="total%d" % g)
             nc.vector.tensor_reduce(out=total[:], in_=p[:], axis=AXIS_X, op=ALU.add)
-            inverse = work.tile([M, bags], F32, name="inverse%d" % c)
+            inverse = keep.tile([M, bags], F32, name="inverse%d" % g)
             nc.vector.reciprocal(out=inverse[:], in_=total[:])
-            weights = work.tile([M, bags, BAG], F32, name="weights%d" % c)
-            piece_bags = PIECE // BAG
-            for low in range(0, bags, piece_bags):
-                piece = slice(low, low + piece_bags)
-                first_slot = starts[c] + low * BAG
-                if first_slot // PIECE < SCALAR_PIECES:
-                    factor = work.tile([M, piece_bags], F32, name="factor%d" % c)
-                    nc.scalar.activation(out=factor[:], in_=inverse[:, piece], func=ACT.Copy, scale=float(BAG))
-                    for g in range(piece_bags):
-                        nc.scalar.activation(
-                            out=weights[:, low + g, :], in_=p[:, low + g, :], func=ACT.Copy, scale=factor[:, g : g + 1]
-                        )
-                else:
-                    nc.vector.scalar_tensor_tensor(
-                        out=weights[:, piece, :],
-                        in0=p[:, piece, :],
-                        scalar=float(BAG),
-                        in1=inverse[:, piece].unsqueeze(2).to_broadcast([M, piece_bags, BAG]),
-                        op0=ALU.mult,
-                        op1=ALU.mult,
-                    )
-                nc.sync.dma_start(
-                    out=out[:, first_slot : first_slot + PIECE],
-                    in_=weights[:, piece, :].rearrange("m g e -> m (g e)"),
-                )
+            weights = keep.tile([M, bags, BAG], F32, name="weights%d" % g)
+            nc.vector.scalar_tensor_tensor(
+                out=weights[:],
+                in0=p[:],
+                scalar=float(BAG),
+                in1=inverse[:].unsqueeze(2).to_broadcast([M, bags, BAG]),
+                op0=ALU.mult,
+                op1=ALU.mult,
+            )
+            first_slot = starts[GROUPS[g][0]]
+            nc.sync.dma_start(
+                out=out[:, first_slot : first_slot + width], in_=weights[:].rearrange("m g e -> m (g e)")
+            )
 
-        below_a = shift(0, score_chunk(0))
-        logits_b = score_chunk(1)
-        logits_c = score_chunk(2)
-        p_a = exponentiate(0, below_a, "x_rows2")
-        p_b = exponentiate(1, shift(1, logits_b), "x_rows1")
-        p_c = exponentiate(2, shift(2, logits_c), "x_rows0")
-        for c, p in enumerate((p_a, p_b, p_c)):
-            normalise(c, p)
+        values = [value(0)]
+        tanh2 = gate_tanh(2, "gate_tanh2", None)
+        values.append(value(1))
+        gates.append(gate(2, tanh2, gate_tiles[2]))
+        values.append(value(2))
+        tanh3 = gate_tanh(3, "gate_tanh3", None)
+        gates.append(gate(3, tanh3, gate_tiles[3]))
+        values.extend(value(c) for c in range(3, len(PIECES)))
+        all_logits = []
+        for g, group in enumerate(GROUPS):
+            logits = psum.tile([M, sum(PIECES[c] for c in group)], F32, name="logits%d" % g)
+            for c in group:
+                at = starts[c] - starts[group[0]]
+                score_piece(c, logits[:, at : at + PIECES[c]])
+            all_logits.append(logits[:])
+        for g, logits in enumerate(all_logits):
+            softmax(g, logits)

@@ -26,6 +26,7 @@ WU_VECTOR_COLS = 70
 WV_VECTOR_COLS = 92
 RUN = 4
 SCALAR_GATES = (3,)
+GPSIMD_GROUPS = 2
 
 FLOPS = 2 * (2 * K * F * SLOTS + F * M * SLOTS)
 
@@ -171,7 +172,7 @@ def tile_attend_milweights_kernel(tc, inst_words, inst_scales, wv, wu, gain, sco
         def score_piece(c, logits):
             width = PIECES[c]
             quarter, at = divmod(starts[c], QUARTER)
-            x_packed = keep.tile([P, width, PACK], BF16, name="x_packed%d" % c, align_bytes=64)
+            x_packed = keep.tile([P, width, PACK], BF16, name="x_packed%d" % c, tag="x_packed%d" % c, align_bytes=64)
             nc.vector.tensor_tensor(
                 out=x_packed[:].rearrange("p (c i) t -> p c t i", i=RUN),
                 in0=gates[quarter][:, :, at : at + width].rearrange("p t (c i) -> p c t i", i=RUN),
@@ -211,15 +212,28 @@ def tile_attend_milweights_kernel(tc, inst_words, inst_scales, wv, wu, gain, sco
             nc.vector.tensor_reduce(out=total[:], in_=p[:], axis=AXIS_X, op=ALU.add)
             inverse = keep.tile([M, bags], F32, name="inverse%d" % g)
             nc.vector.reciprocal(out=inverse[:], in_=total[:])
-            weights = keep.tile([M, bags, BAG], F32, name="weights%d" % g)
-            nc.vector.scalar_tensor_tensor(
-                out=weights[:],
-                in0=p[:],
-                scalar=float(BAG),
-                in1=inverse[:].unsqueeze(2).to_broadcast([M, bags, BAG]),
-                op0=ALU.mult,
-                op1=ALU.mult,
-            )
+            tag = "x_packed%d" % (len(PIECES) - 1) if g == 0 else "weights%d" % g
+            weights = keep.tile([M, bags, BAG], F32, name="weights%d" % g, tag=tag, align_bytes=64)
+            if g < GPSIMD_GROUPS:
+                factor = keep.tile([M, bags], F32, name="factor%d" % g)
+                nc.gpsimd.tensor_scalar(
+                    out=factor[:], in0=inverse[:], scalar1=float(BAG), scalar2=0.0, op0=ALU.mult, op1=ALU.add
+                )
+                nc.gpsimd.tensor_tensor(
+                    out=weights[:],
+                    in0=p[:],
+                    in1=factor[:].unsqueeze(2).to_broadcast([M, bags, BAG]),
+                    op=ALU.mult,
+                )
+            else:
+                nc.vector.scalar_tensor_tensor(
+                    out=weights[:],
+                    in0=p[:],
+                    scalar=float(BAG),
+                    in1=inverse[:].unsqueeze(2).to_broadcast([M, bags, BAG]),
+                    op0=ALU.mult,
+                    op1=ALU.mult,
+                )
             first_slot = starts[GROUPS[g][0]]
             nc.sync.dma_start(
                 out=out[:, first_slot : first_slot + width], in_=weights[:].rearrange("m g e -> m (g e)")

@@ -18,15 +18,15 @@ PACK = 4
 K, T, SLOTS, F, M = 512, 2048, 1024, 512, 128
 BAG = 16
 BANK = 512
-QUARTER = 256
+HALF = SLOTS // 2
 PIECES = (256, 256, 256, 128, 128)
 GROUPS = ((0, 1), (2,), (3, 4))
-PROJ_BANKS = 4
-WU_VECTOR_COLS = 70
-WV_VECTOR_COLS = 92
+PROJ_BANKS = 5
 RUN = 4
-SCALAR_GATES = (3,)
-GPSIMD_GROUPS = 2
+SCALAR_GATE_TILES = 0
+WU_SPLIT = 256
+WV_SPLIT = 192
+SCALAR_SCALED_GROUPS = 1
 
 FLOPS = 2 * (2 * K * F * SLOTS + F * M * SLOTS)
 
@@ -41,24 +41,27 @@ def tile_attend_milweights_kernel(tc, inst_words, inst_scales, wv, wu, gain, sco
         pool_scales = keep.tile([P, T], U8, name="pool_scales", align_bytes=64)
         pool_words = keep.tile([P, T], U32, name="pool_words", align_bytes=64)
         gains = keep.tile([P, PACK], F32, name="gains")
-        wu_raw = keep.tile([P, PACK, F], F32, name="wu_raw")
-        wv_raw = keep.tile([P, PACK, F], F32, name="wv_raw", tag="wv_raw")
+        wu_raw = [keep.tile([P, PACK, w], F32, name="wu_raw%d" % h) for h, w in enumerate((WU_SPLIT, F - WU_SPLIT))]
+        wv_raw = [
+            keep.tile([P, PACK, w], F32, name="wv_raw%d" % h, tag="wv_raw%d" % h)
+            for h, w in enumerate((WV_SPLIT, F - WV_SPLIT))
+        ]
         score_raw = keep.tile([P, PACK, M], F32, name="score_raw")
 
-        nc.sync.dma_start(offsets[:], offs)
         wu_rows = wu.rearrange("(p j) f -> p j f", j=PACK)
-        nc.sync.dma_start(out=wu_raw[:, :2, :], in_=wu_rows[:, :2, :])
+        wv_rows = wv.rearrange("(p j) f -> p j f", j=PACK)
+        word_rows = inst_words[0].rearrange("p n t -> p (n t)").bitcast(I32)
+        nc.sync.dma_start(offsets[:], offs)
+        nc.sync.dma_start(out=wu_raw[0][:], in_=wu_rows[:, :, :WU_SPLIT])
         nc.vector.memset(pool_scales[:].bitcast(I32), 0)
         for r in range(4):
             nc.sync.dma_start(
                 out=pool_scales[r:P:32, :].bitcast(I32), in_=inst_scales[0, r:16:4, :].bitcast(I32)
             )
-        nc.sync.dma_start(out=wu_raw[:, 2:, :], in_=wu_rows[:, 2:, :])
-        nc.sync.dma_start(
-            out=pool_words[:].bitcast(I32),
-            in_=inst_words[0].rearrange("p n t -> p (n t)").bitcast(I32),
-        )
-        nc.sync.dma_start(out=wv_raw[:], in_=wv.rearrange("(p j) f -> p j f", j=PACK))
+        nc.sync.dma_start(out=wu_raw[1][:], in_=wu_rows[:, :, WU_SPLIT:])
+        nc.sync.dma_start(out=pool_words[:].bitcast(I32), in_=word_rows)
+        nc.sync.dma_start(out=wv_raw[0][:], in_=wv_rows[:, :, :WV_SPLIT])
+        nc.sync.dma_start(out=wv_raw[1][:], in_=wv_rows[:, :, WV_SPLIT:])
         nc.sync.dma_start(out=gains[:], in_=gain.rearrange("(p t) o -> p (t o)", t=PACK))
         nc.sync.dma_start(out=score_raw[:], in_=score.rearrange("(p j) m -> p j m", j=PACK))
 
@@ -72,16 +75,18 @@ def tile_attend_milweights_kernel(tc, inst_words, inst_scales, wv, wu, gain, sco
         def gather(pool, dtype, low, high, name, tag):
             picked = keep.tile([P, high - low], dtype, name=name, tag=tag, align_bytes=64)
             nc.vector.tensor_copy(picked[:], pool[:].indirect(offsets[:, low // 16 : high // 16]))
-            return [picked[:, at : at + QUARTER] for at in range(0, high - low, QUARTER)]
+            return picked
 
-        def quantise_projection(raw, vector_cols, name):
+        def quantise_projection(raw, copies, name):
             dealt = keep.tile([P, PACK, P, PACK], BF16, name=name + "_dealt", tag=name + "_dealt", align_bytes=64)
             codes = keep.tile([P, F], U32, name=name + "_codes", align_bytes=64)
             scales = keep.tile([P, F], U8, name=name + "_scales", align_bytes=64)
-            src = raw[:].rearrange("p j (m t) -> p m j t", t=PACK)
             dst = dealt[:].rearrange("p t m j -> p m j t")
-            nc.scalar.copy(out=dst[:, vector_cols:], in_=src[:, vector_cols:])
-            nc.vector.tensor_copy(out=dst[:, :vector_cols], in_=src[:, :vector_cols])
+            low = 0
+            for part, copy in zip(raw, copies):
+                high = low + part.shape[2] // PACK
+                copy(out=dst[:, low:high], in_=part[:].rearrange("p j (m t) -> p m j t", t=PACK))
+                low = high
             nc.vector.quantize_mx(
                 out=codes[:].bitcast(FP8X4), scales=scales[:], in_=dealt[:].rearrange("p t m j -> p (t m j)")
             )
@@ -92,7 +97,7 @@ def tile_attend_milweights_kernel(tc, inst_words, inst_scales, wv, wu, gain, sco
 
         def project(weights, scale, low, width, result):
             codes, scales = weights
-            quarter, at = divmod(low, QUARTER)
+            half, at = divmod(low, HALF)
             per_bank = BANK // width
             for first in range(0, PACK, per_bank):
                 bank = ring[turn[0] % PROJ_BANKS][:].rearrange("p (u i) -> p u i", u=per_bank)
@@ -103,22 +108,22 @@ def tile_attend_milweights_kernel(tc, inst_words, inst_scales, wv, wu, gain, sco
                         out=bank[:, u, :],
                         lhsT=codes[:, cols].bitcast(FP8X4),
                         lhsT_scale=scales[:, cols],
-                        rhs=inst_w[quarter][:, at : at + width].bitcast(FP8X4),
-                        rhs_scale=inst_s[quarter][:, at : at + width],
+                        rhs=inst_w[half][:, at : at + width].bitcast(FP8X4),
+                        rhs_scale=inst_s[:, low : low + width],
                         start=True,
                         stop=True,
                     )
                 nc.scalar.activation(out=result[:, first : first + per_bank, :], in_=bank, func=ACT.Tanh, scale=scale)
 
-        def gate_tanh(q, tag, align):
-            result = keep.tile([P, PACK, QUARTER], F32, name="gate_tanh%d" % q, tag=tag, align_bytes=align)
-            project(wu_mx, 0.5, q * QUARTER, QUARTER, result)
+        def gate_tanh(half, tag):
+            result = keep.tile([P, PACK, HALF], F32, name="gate_tanh%d" % half, tag=tag)
+            project(wu_mx, 0.5, half * HALF, HALF, result)
             return result
 
-        def gate(q, tanh_half, result):
+        def gate(tanh_half, result, scalar_tiles):
             for t in range(PACK):
                 factor = half_gains[:, t : t + 1]
-                if q in SCALAR_GATES:
+                if t < scalar_tiles:
                     nc.scalar.activation(
                         out=result[:, t, :], in_=tanh_half[:, t, :], func=ACT.Identity, scale=factor, bias=factor
                     )
@@ -140,54 +145,53 @@ def tile_attend_milweights_kernel(tc, inst_words, inst_scales, wv, wu, gain, sco
             project(wv_mx, 1.0, starts[c], PIECES[c], result)
             return result
 
-        early = SLOTS - QUARTER
-        inst_s = gather(pool_scales, U8, 0, early, "early_scales", "early_scales")
-        wu_mx = quantise_projection(wu_raw, WU_VECTOR_COLS, "wu")
-        inst_w = gather(pool_words, U32, 0, QUARTER, "first_words", "first_words")
-        inst_w.extend(gather(pool_words, U32, QUARTER, SLOTS, "later_words", "wu_dealt"))
-        tanh0 = gate_tanh(0, "gate_tanh0", 64)
-        wv_mx = quantise_projection(wv_raw, WV_VECTOR_COLS, "wv")
-        tanh1 = gate_tanh(1, "wv_raw", None)
-        after_wv = keep.tile([P, PACK * QUARTER + PACK * M // 2], F32, name="after_wv", tag="wv_dealt", align_bytes=64)
-        gate_tiles = [after_wv[:, : PACK * QUARTER].rearrange("p (t i) -> p t i", t=PACK)]
-        for q in range(1, SLOTS // QUARTER):
-            gate_tiles.append(keep.tile([P, PACK, QUARTER], F32, name="gate%d" % q)[:])
-        gates = [gate(0, tanh0, gate_tiles[0])]
-        inst_s.extend(gather(pool_scales, U8, early, SLOTS, "late_scales", "gate_tanh0"))
-        gates.append(gate(1, tanh1, gate_tiles[1]))
+        inst_s = gather(pool_scales, U8, 0, SLOTS, "inst_s", "inst_s")
+        wu_mx = quantise_projection(wu_raw, (nc.scalar.copy, nc.scalar.copy), "wu")
+        inst_w = [
+            gather(pool_words, U32, 0, HALF, "first_words", "first_words"),
+            gather(pool_words, U32, HALF, SLOTS, "later_words", "wu_dealt"),
+        ]
+        wv_mx = quantise_projection(wv_raw, (nc.scalar.copy, nc.vector.tensor_copy), "wv")
+        tanh0 = gate_tanh(0, "wv_raw0")
+        after_wv = keep.tile([P, PACK * HALF + PACK * M // 2], F32, name="after_wv", tag="wv_dealt", align_bytes=64)
 
-        score_packed = after_wv[:, PACK * QUARTER :].bitcast(BF16).rearrange("p (m j) -> p m j", j=PACK)
+        score_packed = after_wv[:, PACK * HALF :].bitcast(BF16).rearrange("p (m j) -> p m j", j=PACK)
         score_codes = keep.tile([P, M], U32, name="score_codes", align_bytes=64)
         score_scales = keep.tile([P, M], U8, name="score_scales", align_bytes=64)
         nc.vector.tensor_copy(
             out=score_packed.rearrange("p (c i) j -> p c j i", i=4),
             in_=score_raw[:].rearrange("p j (c i) -> p c j i", i=4),
         )
+        gates = [gate(tanh0, after_wv[:, : PACK * HALF].rearrange("p (t i) -> p t i", t=PACK), 0)]
         nc.vector.quantize_mx(
             out=score_codes[:].bitcast(FP8X4),
             scales=score_scales[:],
             in_=score_packed.rearrange("p m j -> p (m j)"),
         )
 
-        def score_piece(c, logits):
-            width = PIECES[c]
-            quarter, at = divmod(starts[c], QUARTER)
-            x_packed = keep.tile([P, width, PACK], BF16, name="x_packed%d" % c, tag="x_packed%d" % c, align_bytes=64)
-            nc.vector.tensor_tensor(
-                out=x_packed[:].rearrange("p (c i) t -> p c t i", i=RUN),
-                in0=gates[quarter][:, :, at : at + width].rearrange("p t (c i) -> p c t i", i=RUN),
-                in1=values[c][:].rearrange("p t (c i) -> p c t i", i=RUN),
-                op=ALU.mult,
-            )
-            x_codes = keep.tile([P, width], U32, name="x_codes%d" % c, align_bytes=64)
-            x_scales = keep.tile([P, width], U8, name="x_scales%d" % c, align_bytes=64)
+        def score_group(g):
+            group = GROUPS[g]
+            total_width = sum(PIECES[c] for c in group)
+            x_packed = keep.tile([P, total_width, PACK], BF16, name="x_packed%d" % g, align_bytes=64)
+            for c in group:
+                half, at = divmod(starts[c], HALF)
+                low = starts[c] - starts[group[0]]
+                nc.vector.tensor_tensor(
+                    out=x_packed[:, low : low + PIECES[c], :].rearrange("p (c i) t -> p c t i", i=RUN),
+                    in0=gates[half][:, :, at : at + PIECES[c]].rearrange("p t (c i) -> p c t i", i=RUN),
+                    in1=values[c][:].rearrange("p t (c i) -> p c t i", i=RUN),
+                    op=ALU.mult,
+                )
+            x_codes = keep.tile([P, total_width], U32, name="x_codes%d" % g, align_bytes=64)
+            x_scales = keep.tile([P, total_width], U8, name="x_scales%d" % g, align_bytes=64)
             nc.vector.quantize_mx(
                 out=x_codes[:].bitcast(FP8X4),
                 scales=x_scales[:],
                 in_=x_packed[:].rearrange("p i t -> p (i t)"),
             )
+            logits = psum.tile([M, total_width], F32, name="logits%d" % g)
             nc.tensor.matmul_mx(
-                out=logits,
+                out=logits[:],
                 lhsT=score_codes[:].bitcast(FP8X4),
                 lhsT_scale=score_scales[:],
                 rhs=x_codes[:].bitcast(FP8X4),
@@ -195,36 +199,38 @@ def tile_attend_milweights_kernel(tc, inst_words, inst_scales, wv, wu, gain, sco
                 start=True,
                 stop=True,
             )
+            return logits[:].rearrange("m (g e) -> m g e", e=BAG)
 
-        def softmax(g, logits):
-            width = sum(PIECES[c] for c in GROUPS[g])
-            bags = width // BAG
-            by_bag = logits.rearrange("m (g e) -> m g e", e=BAG)
+        def exponentiate(g, logits):
+            bags = logits.shape[1]
             top = keep.tile([M, bags], F32, name="top%d" % g)
-            nc.vector.tensor_reduce(out=top[:], in_=by_bag, axis=AXIS_X, op=ALU.max)
+            nc.vector.tensor_reduce(out=top[:], in_=logits, axis=AXIS_X, op=ALU.max)
             below = keep.tile([M, bags, BAG], F32, name="below%d" % g)
             nc.vector.tensor_tensor(
-                out=below[:], in0=by_bag, in1=top[:].unsqueeze(2).to_broadcast([M, bags, BAG]), op=ALU.subtract
+                out=below[:], in0=logits, in1=top[:].unsqueeze(2).to_broadcast([M, bags, BAG]), op=ALU.subtract
             )
             p = keep.tile([M, bags, BAG], F32, name="p%d" % g)
             nc.scalar.activation(out=p[:], in_=below[:], func=ACT.Exp)
+            return p
+
+        def invert(g, p):
+            bags = p.shape[1]
             total = keep.tile([M, bags], F32, name="total%d" % g)
             nc.vector.tensor_reduce(out=total[:], in_=p[:], axis=AXIS_X, op=ALU.add)
             inverse = keep.tile([M, bags], F32, name="inverse%d" % g)
             nc.vector.reciprocal(out=inverse[:], in_=total[:])
-            tag = "x_packed%d" % (len(PIECES) - 1) if g == 0 else "weights%d" % g
-            weights = keep.tile([M, bags, BAG], F32, name="weights%d" % g, tag=tag, align_bytes=64)
-            if g < GPSIMD_GROUPS:
+            return inverse
+
+        def normalise(g, p, inverse):
+            bags = p.shape[1]
+            weights = keep.tile([M, bags, BAG], F32, name="weights%d" % g)
+            if g < SCALAR_SCALED_GROUPS:
                 factor = keep.tile([M, bags], F32, name="factor%d" % g)
-                nc.gpsimd.tensor_scalar(
-                    out=factor[:], in0=inverse[:], scalar1=float(BAG), scalar2=0.0, op0=ALU.mult, op1=ALU.add
-                )
-                nc.gpsimd.tensor_tensor(
-                    out=weights[:],
-                    in0=p[:],
-                    in1=factor[:].unsqueeze(2).to_broadcast([M, bags, BAG]),
-                    op=ALU.mult,
-                )
+                nc.scalar.activation(out=factor[:], in_=inverse[:], func=ACT.Copy, scale=float(BAG))
+                for b in range(bags):
+                    nc.scalar.activation(
+                        out=weights[:, b, :], in_=p[:, b, :], func=ACT.Copy, scale=factor[:, b : b + 1]
+                    )
             else:
                 nc.vector.scalar_tensor_tensor(
                     out=weights[:],
@@ -236,23 +242,18 @@ def tile_attend_milweights_kernel(tc, inst_words, inst_scales, wv, wu, gain, sco
                 )
             first_slot = starts[GROUPS[g][0]]
             nc.sync.dma_start(
-                out=out[:, first_slot : first_slot + width], in_=weights[:].rearrange("m g e -> m (g e)")
+                out=out[:, first_slot : first_slot + bags * BAG], in_=weights[:].rearrange("m g e -> m (g e)")
             )
 
-        values = [value(0)]
-        tanh2 = gate_tanh(2, "gate_tanh2", None)
-        values.append(value(1))
-        gates.append(gate(2, tanh2, gate_tiles[2]))
-        values.append(value(2))
-        tanh3 = gate_tanh(3, "gate_tanh3", None)
-        gates.append(gate(3, tanh3, gate_tiles[3]))
-        values.extend(value(c) for c in range(3, len(PIECES)))
-        all_logits = []
-        for g, group in enumerate(GROUPS):
-            logits = psum.tile([M, sum(PIECES[c] for c in group)], F32, name="logits%d" % g)
-            for c in group:
-                at = starts[c] - starts[group[0]]
-                score_piece(c, logits[:, at : at + PIECES[c]])
-            all_logits.append(logits[:])
-        for g, logits in enumerate(all_logits):
-            softmax(g, logits)
+        values = [value(0), value(1)]
+        tanh1 = gate_tanh(1, "gate_tanh1")
+        gate1 = keep.tile([P, PACK, HALF], F32, name="gate1")
+        gates.append(gate(tanh1, gate1[:], SCALAR_GATE_TILES))
+        values.extend(value(c) for c in range(2, len(PIECES)))
+        p0 = exponentiate(0, score_group(0))
+        inverse0 = invert(0, p0)
+        later = [score_group(g) for g in range(1, len(GROUPS))]
+        ps = [p0] + [exponentiate(g + 1, logits) for g, logits in enumerate(later)]
+        inverses = [inverse0] + [invert(g, ps[g]) for g in range(1, len(GROUPS))]
+        for g in reversed(range(len(GROUPS))):
+            normalise(g, ps[g], inverses[g])

@@ -23,9 +23,9 @@ PIECES = (256, 256, 256, 128, 128)
 GROUPS = ((0, 1), (2,), (3, 4))
 PROJ_BANKS = 5
 RUN = 4
-SCALAR_GATE_TILES = 0
-WU_SPLIT = 256
-WV_SPLIT = 192
+SPLIT = F // 2
+WV_SCALAR_COLS = 46
+SHARED_COLS = 128
 SCALAR_SCALED_GROUPS = 1
 
 FLOPS = 2 * (2 * K * F * SLOTS + F * M * SLOTS)
@@ -41,28 +41,26 @@ def tile_attend_milweights_kernel(tc, inst_words, inst_scales, wv, wu, gain, sco
         pool_scales = keep.tile([P, T], U8, name="pool_scales", align_bytes=64)
         pool_words = keep.tile([P, T], U32, name="pool_words", align_bytes=64)
         gains = keep.tile([P, PACK], F32, name="gains")
-        wu_raw = [keep.tile([P, PACK, w], F32, name="wu_raw%d" % h) for h, w in enumerate((WU_SPLIT, F - WU_SPLIT))]
-        wv_raw = [
-            keep.tile([P, PACK, w], F32, name="wv_raw%d" % h, tag="wv_raw%d" % h)
-            for h, w in enumerate((WV_SPLIT, F - WV_SPLIT))
-        ]
+        wu_raw = [keep.tile([P, PACK, SPLIT], F32, name="wu_raw%d" % h)[:] for h in range(2)]
+        shared = keep.tile([P, PACK, HALF + SPLIT - SHARED_COLS], F32, name="shared")
+        wv_raw = [shared[:, :, HALF - SHARED_COLS :], keep.tile([P, PACK, SPLIT], F32, name="wv_raw1")[:]]
         score_raw = keep.tile([P, PACK, M], F32, name="score_raw")
 
         wu_rows = wu.rearrange("(p j) f -> p j f", j=PACK)
         wv_rows = wv.rearrange("(p j) f -> p j f", j=PACK)
         word_rows = inst_words[0].rearrange("p n t -> p (n t)").bitcast(I32)
         nc.sync.dma_start(offsets[:], offs)
-        nc.sync.dma_start(out=wu_raw[0][:], in_=wu_rows[:, :, :WU_SPLIT])
+        nc.sync.dma_start(out=wu_raw[0], in_=wu_rows[:, :, :SPLIT])
         nc.vector.memset(pool_scales[:].bitcast(I32), 0)
         for r in range(4):
             nc.sync.dma_start(
                 out=pool_scales[r:P:32, :].bitcast(I32), in_=inst_scales[0, r:16:4, :].bitcast(I32)
             )
-        nc.sync.dma_start(out=wu_raw[1][:], in_=wu_rows[:, :, WU_SPLIT:])
+        nc.sync.dma_start(out=wu_raw[1], in_=wu_rows[:, :, SPLIT:])
         nc.sync.dma_start(out=pool_words[:].bitcast(I32), in_=word_rows)
-        nc.sync.dma_start(out=wv_raw[0][:], in_=wv_rows[:, :, :WV_SPLIT])
-        nc.sync.dma_start(out=wv_raw[1][:], in_=wv_rows[:, :, WV_SPLIT:])
         nc.sync.dma_start(out=gains[:], in_=gain.rearrange("(p t) o -> p (t o)", t=PACK))
+        nc.sync.dma_start(out=wv_raw[0], in_=wv_rows[:, :, :SPLIT])
+        nc.sync.dma_start(out=wv_raw[1], in_=wv_rows[:, :, SPLIT:])
         nc.sync.dma_start(out=score_raw[:], in_=score.rearrange("(p j) m -> p j m", j=PACK))
 
         warm = keep.tile([P, 1], F32, name="warm")
@@ -70,23 +68,25 @@ def tile_attend_milweights_kernel(tc, inst_words, inst_scales, wv, wu, gain, sco
         nc.scalar.activation(out=warm[:], in_=warm[:], func=ACT.Tanh)
 
         half_gains = keep.tile([P, PACK], F32, name="half_gains")
-        nc.gpsimd.tensor_scalar(out=half_gains[:], in0=gains[:], scalar1=0.5, scalar2=None, op0=ALU.mult)
+        nc.scalar.activation(out=half_gains[:], in_=gains[:], func=ACT.Copy, scale=0.5)
 
         def gather(pool, dtype, low, high, name, tag):
             picked = keep.tile([P, high - low], dtype, name=name, tag=tag, align_bytes=64)
             nc.vector.tensor_copy(picked[:], pool[:].indirect(offsets[:, low // 16 : high // 16]))
             return picked
 
-        def quantise_projection(raw, copies, name):
+        def quantise_projection(raw, scalar_cols, name):
             dealt = keep.tile([P, PACK, P, PACK], BF16, name=name + "_dealt", tag=name + "_dealt", align_bytes=64)
             codes = keep.tile([P, F], U32, name=name + "_codes", align_bytes=64)
             scales = keep.tile([P, F], U8, name=name + "_scales", align_bytes=64)
             dst = dealt[:].rearrange("p t m j -> p m j t")
-            low = 0
-            for part, copy in zip(raw, copies):
-                high = low + part.shape[2] // PACK
-                copy(out=dst[:, low:high], in_=part[:].rearrange("p j (m t) -> p m j t", t=PACK))
-                low = high
+            for h, cols in enumerate(scalar_cols):
+                src = raw[h].rearrange("p j (m t) -> p m j t", t=PACK)
+                part = dst[:, h * P // 2 : (h + 1) * P // 2]
+                if cols > 0:
+                    nc.scalar.copy(out=part[:, :cols], in_=src[:, :cols])
+                if cols < P // 2:
+                    nc.vector.tensor_copy(out=part[:, cols:], in_=src[:, cols:])
             nc.vector.quantize_mx(
                 out=codes[:].bitcast(FP8X4), scales=scales[:], in_=dealt[:].rearrange("p t m j -> p (t m j)")
             )
@@ -115,15 +115,14 @@ def tile_attend_milweights_kernel(tc, inst_words, inst_scales, wv, wu, gain, sco
                     )
                 nc.scalar.activation(out=result[:, first : first + per_bank, :], in_=bank, func=ACT.Tanh, scale=scale)
 
-        def gate_tanh(half, tag):
-            result = keep.tile([P, PACK, HALF], F32, name="gate_tanh%d" % half, tag=tag)
+        def gate_tanh(half, result):
             project(wu_mx, 0.5, half * HALF, HALF, result)
             return result
 
-        def gate(tanh_half, result, scalar_tiles):
+        def gate(tanh_half, result, on_scalar):
             for t in range(PACK):
                 factor = half_gains[:, t : t + 1]
-                if t < scalar_tiles:
+                if on_scalar:
                     nc.scalar.activation(
                         out=result[:, t, :], in_=tanh_half[:, t, :], func=ACT.Identity, scale=factor, bias=factor
                     )
@@ -146,13 +145,13 @@ def tile_attend_milweights_kernel(tc, inst_words, inst_scales, wv, wu, gain, sco
             return result
 
         inst_s = gather(pool_scales, U8, 0, SLOTS, "inst_s", "inst_s")
-        wu_mx = quantise_projection(wu_raw, (nc.scalar.copy, nc.scalar.copy), "wu")
+        wu_mx = quantise_projection(wu_raw, (P // 2, P // 2), "wu")
         inst_w = [
             gather(pool_words, U32, 0, HALF, "first_words", "first_words"),
             gather(pool_words, U32, HALF, SLOTS, "later_words", "wu_dealt"),
         ]
-        wv_mx = quantise_projection(wv_raw, (nc.scalar.copy, nc.vector.tensor_copy), "wv")
-        tanh0 = gate_tanh(0, "wv_raw0")
+        wv_mx = quantise_projection(wv_raw, (WV_SCALAR_COLS, 0), "wv")
+        tanh0 = gate_tanh(0, shared[:, :, :HALF])
         after_wv = keep.tile([P, PACK * HALF + PACK * M // 2], F32, name="after_wv", tag="wv_dealt", align_bytes=64)
 
         score_packed = after_wv[:, PACK * HALF :].bitcast(BF16).rearrange("p (m j) -> p m j", j=PACK)
@@ -162,7 +161,7 @@ def tile_attend_milweights_kernel(tc, inst_words, inst_scales, wv, wu, gain, sco
             out=score_packed.rearrange("p (c i) j -> p c j i", i=4),
             in_=score_raw[:].rearrange("p j (c i) -> p c j i", i=4),
         )
-        gates = [gate(tanh0, after_wv[:, : PACK * HALF].rearrange("p (t i) -> p t i", t=PACK), 0)]
+        gates = [gate(tanh0, after_wv[:, : PACK * HALF].rearrange("p (t i) -> p t i", t=PACK), False)]
         nc.vector.quantize_mx(
             out=score_codes[:].bitcast(FP8X4),
             scales=score_scales[:],
@@ -246,10 +245,13 @@ def tile_attend_milweights_kernel(tc, inst_words, inst_scales, wv, wu, gain, sco
             )
 
         values = [value(0), value(1)]
-        tanh1 = gate_tanh(1, "gate_tanh1")
+        tanh1 = gate_tanh(1, keep.tile([P, PACK, HALF], F32, name="gate_tanh1")[:])
         gate1 = keep.tile([P, PACK, HALF], F32, name="gate1")
-        gates.append(gate(tanh1, gate1[:], SCALAR_GATE_TILES))
-        values.extend(value(c) for c in range(2, len(PIECES)))
+        gates.append(gate1[:])
+        gate(tanh1[:, :, : PIECES[2]], gate1[:, :, : PIECES[2]], False)
+        values.append(value(2))
+        gate(tanh1[:, :, PIECES[2] :], gate1[:, :, PIECES[2] :], True)
+        values.extend(value(c) for c in range(3, len(PIECES)))
         p0 = exponentiate(0, score_group(0))
         inverse0 = invert(0, p0)
         later = [score_group(g) for g in range(1, len(GROUPS))]

@@ -27,6 +27,7 @@ SPLIT = F // 2
 WV_SCALAR_COLS = 46
 SHARED_COLS = 128
 SCALAR_SCALED_GROUPS = 1
+BAGWISE_GROUP = 1
 
 FLOPS = 2 * (2 * K * F * SLOTS + F * M * SLOTS)
 
@@ -171,7 +172,7 @@ def tile_attend_milweights_kernel(tc, inst_words, inst_scales, wv, wu, gain, sco
         def score_group(g):
             group = GROUPS[g]
             total_width = sum(PIECES[c] for c in group)
-            x_packed = keep.tile([P, total_width, PACK], BF16, name="x_packed%d" % g, align_bytes=64)
+            x_packed = keep.tile([P, total_width, PACK], BF16, name="x_packed%d" % g, tag="x_packed%d" % g, align_bytes=64)
             for c in group:
                 half, at = divmod(starts[c], HALF)
                 low = starts[c] - starts[group[0]]
@@ -202,34 +203,50 @@ def tile_attend_milweights_kernel(tc, inst_words, inst_scales, wv, wu, gain, sco
 
         def exponentiate(g, logits):
             bags = logits.shape[1]
-            top = keep.tile([M, bags], F32, name="top%d" % g)
-            nc.vector.tensor_reduce(out=top[:], in_=logits, axis=AXIS_X, op=ALU.max)
-            below = keep.tile([M, bags, BAG], F32, name="below%d" % g)
-            nc.vector.tensor_tensor(
-                out=below[:], in0=logits, in1=top[:].unsqueeze(2).to_broadcast([M, bags, BAG]), op=ALU.subtract
-            )
+            minus_top = keep.tile([M, bags], F32, name="minus_top%d" % g)
+            nc.vector.tensor_reduce(out=minus_top[:], in_=logits, axis=AXIS_X, op=ALU.max, negate=True)
             p = keep.tile([M, bags, BAG], F32, name="p%d" % g)
-            nc.scalar.activation(out=p[:], in_=below[:], func=ACT.Exp)
-            return p
-
-        def invert(g, p):
-            bags = p.shape[1]
             total = keep.tile([M, bags], F32, name="total%d" % g)
-            nc.vector.tensor_reduce(out=total[:], in_=p[:], axis=AXIS_X, op=ALU.add)
-            inverse = keep.tile([M, bags], F32, name="inverse%d" % g)
+            if g == BAGWISE_GROUP:
+                for b in range(bags):
+                    nc.scalar.activation(
+                        out=p[:, b, :],
+                        in_=logits[:, b, :],
+                        func=ACT.Exp,
+                        bias=minus_top[:, b : b + 1],
+                        accum_out=total[:, b : b + 1],
+                    )
+            else:
+                below = keep.tile([M, bags, BAG], F32, name="below%d" % g)
+                nc.vector.tensor_tensor(
+                    out=below[:],
+                    in0=logits,
+                    in1=minus_top[:].unsqueeze(2).to_broadcast([M, bags, BAG]),
+                    op=ALU.add,
+                )
+                nc.scalar.activation(out=p[:], in_=below[:], func=ACT.Exp)
+            return p, total
+
+        def invert(g, p, total):
+            if g != BAGWISE_GROUP:
+                nc.vector.tensor_reduce(out=total[:], in_=p[:], axis=AXIS_X, op=ALU.add)
+            inverse = keep.tile([M, p.shape[1]], F32, name="inverse%d" % g)
             nc.vector.reciprocal(out=inverse[:], in_=total[:])
             return inverse
 
         def normalise(g, p, inverse):
             bags = p.shape[1]
-            weights = keep.tile([M, bags, BAG], F32, name="weights%d" % g)
+            tag = "x_packed%d" % (len(GROUPS) - 1) if g == 0 else "weights%d" % g
+            weights = keep.tile([M, bags, BAG], F32, name="weights%d" % g, tag=tag, align_bytes=64)
             if g < SCALAR_SCALED_GROUPS:
                 factor = keep.tile([M, bags], F32, name="factor%d" % g)
                 nc.scalar.activation(out=factor[:], in_=inverse[:], func=ACT.Copy, scale=float(BAG))
-                for b in range(bags):
-                    nc.scalar.activation(
-                        out=weights[:, b, :], in_=p[:, b, :], func=ACT.Copy, scale=factor[:, b : b + 1]
-                    )
+                nc.gpsimd.tensor_tensor(
+                    out=weights[:],
+                    in0=p[:],
+                    in1=factor[:].unsqueeze(2).to_broadcast([M, bags, BAG]),
+                    op=ALU.mult,
+                )
             else:
                 nc.vector.scalar_tensor_tensor(
                     out=weights[:],
@@ -253,9 +270,9 @@ def tile_attend_milweights_kernel(tc, inst_words, inst_scales, wv, wu, gain, sco
         gate(tanh1[:, :, PIECES[2] :], gate1[:, :, PIECES[2] :], True)
         values.extend(value(c) for c in range(3, len(PIECES)))
         p0 = exponentiate(0, score_group(0))
-        inverse0 = invert(0, p0)
+        inverse0 = invert(0, *p0)
         later = [score_group(g) for g in range(1, len(GROUPS))]
         ps = [p0] + [exponentiate(g + 1, logits) for g, logits in enumerate(later)]
-        inverses = [inverse0] + [invert(g, ps[g]) for g in range(1, len(GROUPS))]
+        inverses = [inverse0] + [invert(g, *ps[g]) for g in range(1, len(GROUPS))]
         for g in reversed(range(len(GROUPS))):
-            normalise(g, ps[g], inverses[g])
+            normalise(g, ps[g][0], inverses[g])

@@ -26,7 +26,6 @@ RUN = 4
 SPLIT = F // 2
 WV_SCALAR_COLS = 46
 SHARED_COLS = 128
-SCALAR_SCALED_GROUPS = 1
 BAGWISE_GROUP = 1
 
 FLOPS = 2 * (2 * K * F * SLOTS + F * M * SLOTS)
@@ -201,10 +200,13 @@ def tile_attend_milweights_kernel(tc, inst_words, inst_scales, wv, wu, gain, sco
             )
             return logits[:].rearrange("m (g e) -> m g e", e=BAG)
 
-        def exponentiate(g, logits):
-            bags = logits.shape[1]
-            minus_top = keep.tile([M, bags], F32, name="minus_top%d" % g)
+        def maxima(g, logits):
+            minus_top = keep.tile([M, logits.shape[1]], F32, name="minus_top%d" % g)
             nc.vector.tensor_reduce(out=minus_top[:], in_=logits, axis=AXIS_X, op=ALU.max, negate=True)
+            return minus_top
+
+        def exponentiate(g, logits, minus_top):
+            bags = logits.shape[1]
             p = keep.tile([M, bags, BAG], F32, name="p%d" % g)
             total = keep.tile([M, bags], F32, name="total%d" % g)
             if g == BAGWISE_GROUP:
@@ -227,6 +229,32 @@ def tile_attend_milweights_kernel(tc, inst_words, inst_scales, wv, wu, gain, sco
                 nc.scalar.activation(out=p[:], in_=below[:], func=ACT.Exp)
             return p, total
 
+        def store(g, weights):
+            first_slot = starts[GROUPS[g][0]]
+            nc.sync.dma_start(
+                out=out[:, first_slot : first_slot + weights.shape[1] * BAG],
+                in_=weights[:].rearrange("m g e -> m (g e)"),
+            )
+
+        def normalise_on_gpsimd(g, p, inverse):
+            bags = p.shape[1]
+            factor = keep.tile([M, bags], F32, name="factor", tag="x_packed%d" % (len(GROUPS) - 1), align_bytes=64)
+            nc.scalar.activation(out=factor[:], in_=inverse[:], func=ACT.Copy, scale=float(BAG))
+            weights = keep.tile([M, bags, BAG], F32, name="weights%d" % g)
+            nc.gpsimd.tensor_tensor(
+                out=weights[:], in0=p[:], in1=factor[:].unsqueeze(2).to_broadcast([M, bags, BAG]), op=ALU.mult
+            )
+            store(g, weights)
+
+        def normalise_on_scalar(g, p, inverse):
+            bags = p.shape[1]
+            factor = keep.tile([M, bags], F32, name="scalar_factor")
+            nc.scalar.activation(out=factor[:], in_=inverse[:], func=ACT.Copy, scale=float(BAG))
+            weights = keep.tile([M, bags, BAG], F32, name="weights%d" % g)
+            for b in range(bags):
+                nc.scalar.activation(out=weights[:, b, :], in_=p[:, b, :], func=ACT.Copy, scale=factor[:, b : b + 1])
+            store(g, weights)
+
         def invert(g, p, total):
             if g != BAGWISE_GROUP:
                 nc.vector.tensor_reduce(out=total[:], in_=p[:], axis=AXIS_X, op=ALU.add)
@@ -236,30 +264,16 @@ def tile_attend_milweights_kernel(tc, inst_words, inst_scales, wv, wu, gain, sco
 
         def normalise(g, p, inverse):
             bags = p.shape[1]
-            tag = "x_packed%d" % (len(GROUPS) - 1) if g == 0 else "weights%d" % g
-            weights = keep.tile([M, bags, BAG], F32, name="weights%d" % g, tag=tag, align_bytes=64)
-            if g < SCALAR_SCALED_GROUPS:
-                factor = keep.tile([M, bags], F32, name="factor%d" % g)
-                nc.scalar.activation(out=factor[:], in_=inverse[:], func=ACT.Copy, scale=float(BAG))
-                nc.gpsimd.tensor_tensor(
-                    out=weights[:],
-                    in0=p[:],
-                    in1=factor[:].unsqueeze(2).to_broadcast([M, bags, BAG]),
-                    op=ALU.mult,
-                )
-            else:
-                nc.vector.scalar_tensor_tensor(
-                    out=weights[:],
-                    in0=p[:],
-                    scalar=float(BAG),
-                    in1=inverse[:].unsqueeze(2).to_broadcast([M, bags, BAG]),
-                    op0=ALU.mult,
-                    op1=ALU.mult,
-                )
-            first_slot = starts[GROUPS[g][0]]
-            nc.sync.dma_start(
-                out=out[:, first_slot : first_slot + bags * BAG], in_=weights[:].rearrange("m g e -> m (g e)")
+            weights = keep.tile([M, bags, BAG], F32, name="weights%d" % g)
+            nc.vector.scalar_tensor_tensor(
+                out=weights[:],
+                in0=p[:],
+                scalar=float(BAG),
+                in1=inverse[:].unsqueeze(2).to_broadcast([M, bags, BAG]),
+                op0=ALU.mult,
+                op1=ALU.mult,
             )
+            store(g, weights)
 
         values = [value(0), value(1)]
         tanh1 = gate_tanh(1, keep.tile([P, PACK, HALF], F32, name="gate_tanh1")[:])
@@ -269,10 +283,15 @@ def tile_attend_milweights_kernel(tc, inst_words, inst_scales, wv, wu, gain, sco
         values.append(value(2))
         gate(tanh1[:, :, PIECES[2] :], gate1[:, :, PIECES[2] :], True)
         values.extend(value(c) for c in range(3, len(PIECES)))
-        p0 = exponentiate(0, score_group(0))
-        inverse0 = invert(0, *p0)
-        later = [score_group(g) for g in range(1, len(GROUPS))]
-        ps = [p0] + [exponentiate(g + 1, logits) for g, logits in enumerate(later)]
-        inverses = [inverse0] + [invert(g, *ps[g]) for g in range(1, len(GROUPS))]
-        for g in reversed(range(len(GROUPS))):
-            normalise(g, ps[g][0], inverses[g])
+        logits0 = score_group(0)
+        first = exponentiate(0, logits0, maxima(0, logits0))
+        logits1 = score_group(1)
+        logits2 = score_group(2)
+        minus_top1 = maxima(1, logits1)
+        normalise_on_gpsimd(0, first[0], invert(0, *first))
+        third = exponentiate(2, logits2, maxima(2, logits2))
+        second = exponentiate(1, logits1, minus_top1)
+        inverse2 = invert(2, *third)
+        inverse1 = invert(1, *second)
+        normalise(2, third[0], inverse2)
+        normalise_on_scalar(1, second[0], inverse1)

@@ -75,7 +75,7 @@ def tile_attend_milweights_kernel(tc, inst_words, inst_scales, wv, wu, gain, sco
             nc.vector.tensor_copy(picked[:], pool[:].indirect(offsets[:, low // 16 : high // 16]))
             return picked
 
-        def quantise_projection(raw, scalar_cols, name):
+        def quantise_projection(raw, scalar_cols, calls, name):
             dealt = keep.tile([P, PACK, P, PACK], BF16, name=name + "_dealt", tag=name + "_dealt", align_bytes=64)
             codes = keep.tile([P, F], U32, name=name + "_codes", align_bytes=64)
             scales = keep.tile([P, F], U8, name=name + "_scales", align_bytes=64)
@@ -87,9 +87,14 @@ def tile_attend_milweights_kernel(tc, inst_words, inst_scales, wv, wu, gain, sco
                     nc.scalar.copy(out=part[:, :cols], in_=src[:, :cols])
                 if cols < P // 2:
                     nc.vector.tensor_copy(out=part[:, cols:], in_=src[:, cols:])
-            nc.vector.quantize_mx(
-                out=codes[:].bitcast(FP8X4), scales=scales[:], in_=dealt[:].rearrange("p t m j -> p (t m j)")
-            )
+            flat = dealt[:].rearrange("p t m j -> p (t m j)")
+            for low in range(0, F, F // calls):
+                high = low + F // calls
+                nc.vector.quantize_mx(
+                    out=codes[:, low:high].bitcast(FP8X4),
+                    scales=scales[:, low:high],
+                    in_=flat[:, low * PACK : high * PACK],
+                )
             return codes, scales
 
         ring = [psum.tile([P, BANK], F32, name="proj%d" % b) for b in range(PROJ_BANKS)]
@@ -145,23 +150,23 @@ def tile_attend_milweights_kernel(tc, inst_words, inst_scales, wv, wu, gain, sco
             return result
 
         inst_s = gather(pool_scales, U8, 0, SLOTS, "inst_s", "inst_s")
-        wu_mx = quantise_projection(wu_raw, (P // 2, P // 2), "wu")
+        wu_mx = quantise_projection(wu_raw, (P // 2, P // 2), 1, "wu")
         inst_w = [
             gather(pool_words, U32, 0, HALF, "first_words", "first_words"),
             gather(pool_words, U32, HALF, SLOTS, "later_words", "wu_dealt"),
         ]
-        wv_mx = quantise_projection(wv_raw, (WV_SCALAR_COLS, 0), "wv")
+        wv_mx = quantise_projection(wv_raw, (WV_SCALAR_COLS, 0), 2, "wv")
         tanh0 = gate_tanh(0, shared[:, :, :HALF])
-        after_wv = keep.tile([P, PACK * HALF + PACK * M // 2], F32, name="after_wv", tag="wv_dealt", align_bytes=64)
+        gate0 = keep.tile([P, PACK, HALF], F32, name="gate0", tag="wv_dealt", align_bytes=64)
 
-        score_packed = after_wv[:, PACK * HALF :].bitcast(BF16).rearrange("p (m j) -> p m j", j=PACK)
+        score_packed = keep.tile([P, M, PACK], BF16, name="score_packed", align_bytes=64)[:]
         score_codes = keep.tile([P, M], U32, name="score_codes", align_bytes=64)
         score_scales = keep.tile([P, M], U8, name="score_scales", align_bytes=64)
         nc.vector.tensor_copy(
             out=score_packed.rearrange("p (c i) j -> p c j i", i=4),
             in_=score_raw[:].rearrange("p j (c i) -> p c j i", i=4),
         )
-        gates = [gate(tanh0, after_wv[:, : PACK * HALF].rearrange("p (t i) -> p t i", t=PACK), False)]
+        gates = [gate(tanh0, gate0[:], False)]
         nc.vector.quantize_mx(
             out=score_codes[:].bitcast(FP8X4),
             scales=score_scales[:],
@@ -236,16 +241,6 @@ def tile_attend_milweights_kernel(tc, inst_words, inst_scales, wv, wu, gain, sco
                 in_=weights[:].rearrange("m g e -> m (g e)"),
             )
 
-        def normalise_on_gpsimd(g, p, inverse):
-            bags = p.shape[1]
-            factor = keep.tile([M, bags], F32, name="factor", tag="x_packed%d" % (len(GROUPS) - 1), align_bytes=64)
-            nc.scalar.activation(out=factor[:], in_=inverse[:], func=ACT.Copy, scale=float(BAG))
-            weights = keep.tile([M, bags, BAG], F32, name="weights%d" % g)
-            nc.gpsimd.tensor_tensor(
-                out=weights[:], in0=p[:], in1=factor[:].unsqueeze(2).to_broadcast([M, bags, BAG]), op=ALU.mult
-            )
-            store(g, weights)
-
         def normalise_on_scalar(g, p, inverse):
             bags = p.shape[1]
             factor = keep.tile([M, bags], F32, name="scalar_factor")
@@ -288,10 +283,9 @@ def tile_attend_milweights_kernel(tc, inst_words, inst_scales, wv, wu, gain, sco
         logits1 = score_group(1)
         logits2 = score_group(2)
         minus_top1 = maxima(1, logits1)
-        normalise_on_gpsimd(0, first[0], invert(0, *first))
+        inverse0 = invert(0, *first)
         third = exponentiate(2, logits2, maxima(2, logits2))
         second = exponentiate(1, logits1, minus_top1)
-        inverse2 = invert(2, *third)
-        inverse1 = invert(1, *second)
-        normalise(2, third[0], inverse2)
-        normalise_on_scalar(1, second[0], inverse1)
+        normalise(0, first[0], inverse0)
+        normalise_on_scalar(1, second[0], invert(1, *second))
+        normalise(2, third[0], invert(2, *third))

@@ -24,7 +24,8 @@ GROUPS = ((0, 1), (2,), (3, 4))
 PROJ_BANKS = 5
 RUN = 4
 SPLIT = F // 2
-WV_SCALAR_COLS = 46
+WV_SCALAR_COLS = 40
+SCALAR_GATE_TILES = 2
 SHARED_COLS = 128
 BAGWISE_GROUP = 1
 
@@ -62,10 +63,6 @@ def tile_attend_milweights_kernel(tc, inst_words, inst_scales, wv, wu, gain, sco
         nc.sync.dma_start(out=wv_raw[0], in_=wv_rows[:, :, :SPLIT])
         nc.sync.dma_start(out=wv_raw[1], in_=wv_rows[:, :, SPLIT:])
         nc.sync.dma_start(out=score_raw[:], in_=score.rearrange("(p j) m -> p j m", j=PACK))
-
-        warm = keep.tile([P, 1], F32, name="warm")
-        nc.gpsimd.memset(warm[:], 0.0)
-        nc.scalar.activation(out=warm[:], in_=warm[:], func=ACT.Tanh)
 
         half_gains = keep.tile([P, PACK], F32, name="half_gains")
         nc.scalar.activation(out=half_gains[:], in_=gains[:], func=ACT.Copy, scale=0.5)
@@ -120,14 +117,10 @@ def tile_attend_milweights_kernel(tc, inst_words, inst_scales, wv, wu, gain, sco
                     )
                 nc.scalar.activation(out=result[:, first : first + per_bank, :], in_=bank, func=ACT.Tanh, scale=scale)
 
-        def gate_tanh(half, result):
-            project(wu_mx, 0.5, half * HALF, HALF, result)
-            return result
-
-        def gate(tanh_half, result, on_scalar):
+        def gate(tanh_half, result, scalar_tiles):
             for t in range(PACK):
                 factor = half_gains[:, t : t + 1]
-                if on_scalar:
+                if t < scalar_tiles:
                     nc.scalar.activation(
                         out=result[:, t, :], in_=tanh_half[:, t, :], func=ACT.Identity, scale=factor, bias=factor
                     )
@@ -156,7 +149,8 @@ def tile_attend_milweights_kernel(tc, inst_words, inst_scales, wv, wu, gain, sco
             gather(pool_words, U32, HALF, SLOTS, "later_words", "wu_dealt"),
         ]
         wv_mx = quantise_projection(wv_raw, (WV_SCALAR_COLS, 0), 2, "wv")
-        tanh0 = gate_tanh(0, shared[:, :, :HALF])
+        tanh0 = shared[:, :, :HALF]
+        project(wu_mx, 0.5, 0, HALF, tanh0)
         gate0 = keep.tile([P, PACK, HALF], F32, name="gate0", tag="wv_dealt", align_bytes=64)
 
         score_packed = keep.tile([P, M, PACK], BF16, name="score_packed", align_bytes=64)[:]
@@ -166,7 +160,7 @@ def tile_attend_milweights_kernel(tc, inst_words, inst_scales, wv, wu, gain, sco
             out=score_packed.rearrange("p (c i) j -> p c j i", i=4),
             in_=score_raw[:].rearrange("p j (c i) -> p c j i", i=4),
         )
-        gates = [gate(tanh0, gate0[:], False)]
+        gates = [gate(tanh0, gate0[:], 0)]
         nc.vector.quantize_mx(
             out=score_codes[:].bitcast(FP8X4),
             scales=score_scales[:],
@@ -241,15 +235,6 @@ def tile_attend_milweights_kernel(tc, inst_words, inst_scales, wv, wu, gain, sco
                 in_=weights[:].rearrange("m g e -> m (g e)"),
             )
 
-        def normalise_on_scalar(g, p, inverse):
-            bags = p.shape[1]
-            factor = keep.tile([M, bags], F32, name="scalar_factor")
-            nc.scalar.activation(out=factor[:], in_=inverse[:], func=ACT.Copy, scale=float(BAG))
-            weights = keep.tile([M, bags, BAG], F32, name="weights%d" % g)
-            for b in range(bags):
-                nc.scalar.activation(out=weights[:, b, :], in_=p[:, b, :], func=ACT.Copy, scale=factor[:, b : b + 1])
-            store(g, weights)
-
         def invert(g, p, total):
             if g != BAGWISE_GROUP:
                 nc.vector.tensor_reduce(out=total[:], in_=p[:], axis=AXIS_X, op=ALU.add)
@@ -271,12 +256,16 @@ def tile_attend_milweights_kernel(tc, inst_words, inst_scales, wv, wu, gain, sco
             store(g, weights)
 
         values = [value(0), value(1)]
-        tanh1 = gate_tanh(1, keep.tile([P, PACK, HALF], F32, name="gate_tanh1")[:])
+        tanh1 = keep.tile([P, PACK, HALF], F32, name="gate_tanh1")
         gate1 = keep.tile([P, PACK, HALF], F32, name="gate1")
         gates.append(gate1[:])
-        gate(tanh1[:, :, : PIECES[2]], gate1[:, :, : PIECES[2]], False)
+        third = slice(0, PIECES[2])
+        last = slice(PIECES[2], HALF)
+        project(wu_mx, 0.5, HALF, PIECES[2], tanh1[:, :, third])
+        gate(tanh1[:, :, third], gate1[:, :, third], 0)
         values.append(value(2))
-        gate(tanh1[:, :, PIECES[2] :], gate1[:, :, PIECES[2] :], True)
+        project(wu_mx, 0.5, HALF + PIECES[2], HALF - PIECES[2], tanh1[:, :, last])
+        gate(tanh1[:, :, last], gate1[:, :, last], SCALAR_GATE_TILES)
         values.extend(value(c) for c in range(3, len(PIECES)))
         logits0 = score_group(0)
         first = exponentiate(0, logits0, maxima(0, logits0))
@@ -284,8 +273,10 @@ def tile_attend_milweights_kernel(tc, inst_words, inst_scales, wv, wu, gain, sco
         logits2 = score_group(2)
         minus_top1 = maxima(1, logits1)
         inverse0 = invert(0, *first)
-        third = exponentiate(2, logits2, maxima(2, logits2))
+        fourth = exponentiate(2, logits2, maxima(2, logits2))
         second = exponentiate(1, logits1, minus_top1)
         normalise(0, first[0], inverse0)
-        normalise_on_scalar(1, second[0], invert(1, *second))
-        normalise(2, third[0], invert(2, *third))
+        inverse2 = invert(2, *fourth)
+        inverse1 = invert(1, *second)
+        normalise(1, second[0], inverse1)
+        normalise(2, fourth[0], inverse2)

@@ -25,7 +25,7 @@ PROJ_BANKS = 5
 RUN = 4
 SPLIT = F // 2
 WV_SCALAR_COLS = 40
-SCALAR_GATE_TILES = 2
+SCALAR_GATE_TILES = 3
 SHARED_COLS = 128
 BAGWISE_GROUP = 1
 
@@ -228,13 +228,6 @@ def tile_attend_milweights_kernel(tc, inst_words, inst_scales, wv, wu, gain, sco
                 nc.scalar.activation(out=p[:], in_=below[:], func=ACT.Exp)
             return p, total
 
-        def store(g, weights):
-            first_slot = starts[GROUPS[g][0]]
-            nc.sync.dma_start(
-                out=out[:, first_slot : first_slot + weights.shape[1] * BAG],
-                in_=weights[:].rearrange("m g e -> m (g e)"),
-            )
-
         def invert(g, p, total):
             if g != BAGWISE_GROUP:
                 nc.vector.tensor_reduce(out=total[:], in_=p[:], axis=AXIS_X, op=ALU.add)
@@ -242,18 +235,24 @@ def tile_attend_milweights_kernel(tc, inst_words, inst_scales, wv, wu, gain, sco
             nc.vector.reciprocal(out=inverse[:], in_=total[:])
             return inverse
 
-        def normalise(g, p, inverse):
-            bags = p.shape[1]
-            weights = keep.tile([M, bags, BAG], F32, name="weights%d" % g)
-            nc.vector.scalar_tensor_tensor(
-                out=weights[:],
-                in0=p[:],
-                scalar=float(BAG),
-                in1=inverse[:].unsqueeze(2).to_broadcast([M, bags, BAG]),
-                op0=ALU.mult,
-                op1=ALU.mult,
-            )
-            store(g, weights)
+        def normalise(g, p, inverse, parts):
+            bags = p.shape[1] // parts
+            weights = keep.tile([M, parts, bags, BAG], F32, name="weights%d" % g)
+            for part in range(parts):
+                some = slice(part * bags, (part + 1) * bags)
+                nc.vector.scalar_tensor_tensor(
+                    out=weights[:, part],
+                    in0=p[:, some, :],
+                    scalar=float(BAG),
+                    in1=inverse[:, some].unsqueeze(2).to_broadcast([M, bags, BAG]),
+                    op0=ALU.mult,
+                    op1=ALU.mult,
+                )
+                first_slot = starts[GROUPS[g][0]] + part * bags * BAG
+                nc.sync.dma_start(
+                    out=out[:, first_slot : first_slot + bags * BAG],
+                    in_=weights[:, part].rearrange("m g e -> m (g e)"),
+                )
 
         values = [value(0), value(1)]
         tanh1 = keep.tile([P, PACK, HALF], F32, name="gate_tanh1")
@@ -275,8 +274,8 @@ def tile_attend_milweights_kernel(tc, inst_words, inst_scales, wv, wu, gain, sco
         inverse0 = invert(0, *first)
         fourth = exponentiate(2, logits2, maxima(2, logits2))
         second = exponentiate(1, logits1, minus_top1)
-        normalise(0, first[0], inverse0)
+        normalise(0, first[0], inverse0, 1)
         inverse2 = invert(2, *fourth)
         inverse1 = invert(1, *second)
-        normalise(1, second[0], inverse1)
-        normalise(2, fourth[0], inverse2)
+        normalise(1, second[0], inverse1, 1)
+        normalise(2, fourth[0], inverse2, 2)

@@ -27,7 +27,7 @@ SPLIT = F // 2
 WV_SCALAR_COLS = 40
 SCALAR_GATE_TILES = 3
 SHARED_COLS = 128
-BAGWISE_GROUP = 1
+BAGWISE_BAGS = (8, 16, 0)
 
 FLOPS = 2 * (2 * K * F * SLOTS + F * M * SLOTS)
 
@@ -208,29 +208,32 @@ def tile_attend_milweights_kernel(tc, inst_words, inst_scales, wv, wu, gain, sco
             bags = logits.shape[1]
             p = keep.tile([M, bags, BAG], F32, name="p%d" % g)
             total = keep.tile([M, bags], F32, name="total%d" % g)
-            if g == BAGWISE_GROUP:
-                for b in range(bags):
-                    nc.scalar.activation(
-                        out=p[:, b, :],
-                        in_=logits[:, b, :],
-                        func=ACT.Exp,
-                        bias=minus_top[:, b : b + 1],
-                        accum_out=total[:, b : b + 1],
-                    )
-            else:
-                below = keep.tile([M, bags, BAG], F32, name="below%d" % g)
+            whole = bags - BAGWISE_BAGS[g]
+            if whole > 0:
+                below = keep.tile([M, whole, BAG], F32, name="below%d" % g)
                 nc.vector.tensor_tensor(
                     out=below[:],
-                    in0=logits,
-                    in1=minus_top[:].unsqueeze(2).to_broadcast([M, bags, BAG]),
+                    in0=logits[:, :whole, :],
+                    in1=minus_top[:, :whole].unsqueeze(2).to_broadcast([M, whole, BAG]),
                     op=ALU.add,
                 )
-                nc.scalar.activation(out=p[:], in_=below[:], func=ACT.Exp)
+                nc.scalar.activation(out=p[:, :whole, :], in_=below[:], func=ACT.Exp)
             return p, total
 
+        def exponentiate_bagwise(g, logits, minus_top, p, total):
+            for b in range(logits.shape[1] - BAGWISE_BAGS[g], logits.shape[1]):
+                nc.scalar.activation(
+                    out=p[:, b, :],
+                    in_=logits[:, b, :],
+                    func=ACT.Exp,
+                    bias=minus_top[:, b : b + 1],
+                    accum_out=total[:, b : b + 1],
+                )
+
         def invert(g, p, total):
-            if g != BAGWISE_GROUP:
-                nc.vector.tensor_reduce(out=total[:], in_=p[:], axis=AXIS_X, op=ALU.add)
+            whole = p.shape[1] - BAGWISE_BAGS[g]
+            if whole > 0:
+                nc.vector.tensor_reduce(out=total[:, :whole], in_=p[:, :whole, :], axis=AXIS_X, op=ALU.add)
             inverse = keep.tile([M, p.shape[1]], F32, name="inverse%d" % g)
             nc.vector.reciprocal(out=inverse[:], in_=total[:])
             return inverse
@@ -267,13 +270,16 @@ def tile_attend_milweights_kernel(tc, inst_words, inst_scales, wv, wu, gain, sco
         gate(tanh1[:, :, last], gate1[:, :, last], SCALAR_GATE_TILES)
         values.extend(value(c) for c in range(3, len(PIECES)))
         logits0 = score_group(0)
-        first = exponentiate(0, logits0, maxima(0, logits0))
+        minus_top0 = maxima(0, logits0)
+        first = exponentiate(0, logits0, minus_top0)
+        exponentiate_bagwise(0, logits0, minus_top0, *first)
         logits1 = score_group(1)
         logits2 = score_group(2)
         minus_top1 = maxima(1, logits1)
         inverse0 = invert(0, *first)
         fourth = exponentiate(2, logits2, maxima(2, logits2))
         second = exponentiate(1, logits1, minus_top1)
+        exponentiate_bagwise(1, logits1, minus_top1, *second)
         normalise(0, first[0], inverse0, 1)
         inverse2 = invert(2, *fourth)
         inverse1 = invert(1, *second)

@@ -19,15 +19,17 @@ K, T, SLOTS, F, M = 512, 2048, 1024, 512, 128
 BAG = 16
 BANK = 512
 HALF = SLOTS // 2
+QUARTER = SLOTS // 4
+
 PIECES = (256, 256, 256, 128, 128)
 GROUPS = ((0, 1), (2,), (3, 4))
 PROJ_BANKS = 5
 RUN = 4
 SPLIT = F // 2
-WV_SCALAR_COLS = 40
+WV_SCALAR_COLS = 46
 SCALAR_GATE_TILES = 3
 SHARED_COLS = 128
-BAGWISE_BAGS = (8, 16, 0)
+BAGWISE_BAGS = (8, 16, 6)
 
 FLOPS = 2 * (2 * K * F * SLOTS + F * M * SLOTS)
 
@@ -67,24 +69,27 @@ def tile_attend_milweights_kernel(tc, inst_words, inst_scales, wv, wu, gain, sco
         half_gains = keep.tile([P, PACK], F32, name="half_gains")
         nc.scalar.activation(out=half_gains[:], in_=gains[:], func=ACT.Copy, scale=0.5)
 
-        def gather(pool, dtype, low, high, name, tag):
+        def gather(pool, dtype, low, high, step, name, tag):
             picked = keep.tile([P, high - low], dtype, name=name, tag=tag, align_bytes=64)
-            nc.vector.tensor_copy(picked[:], pool[:].indirect(offsets[:, low // 16 : high // 16]))
+            for at in range(low, high, step):
+                nc.vector.tensor_copy(
+                    picked[:, at - low : at - low + step], pool[:].indirect(offsets[:, at // 16 : (at + step) // 16])
+                )
             return picked
 
         def quantise_projection(raw, scalar_cols, calls, name):
             dealt = keep.tile([P, PACK, P, PACK], BF16, name=name + "_dealt", tag=name + "_dealt", align_bytes=64)
             codes = keep.tile([P, F], U32, name=name + "_codes", align_bytes=64)
             scales = keep.tile([P, F], U8, name=name + "_scales", align_bytes=64)
-            dst = dealt[:].rearrange("p t m j -> p m j t")
+            dst = dealt[:].rearrange("p t q j -> p q j t")
             for h, cols in enumerate(scalar_cols):
-                src = raw[h].rearrange("p j (m t) -> p m j t", t=PACK)
+                src = raw[h].rearrange("p j (q t) -> p q j t", t=PACK)
                 part = dst[:, h * P // 2 : (h + 1) * P // 2]
                 if cols > 0:
                     nc.scalar.copy(out=part[:, :cols], in_=src[:, :cols])
                 if cols < P // 2:
                     nc.vector.tensor_copy(out=part[:, cols:], in_=src[:, cols:])
-            flat = dealt[:].rearrange("p t m j -> p (t m j)")
+            flat = dealt[:].rearrange("p t q j -> p (t q j)")
             for low in range(0, F, F // calls):
                 high = low + F // calls
                 nc.vector.quantize_mx(
@@ -95,45 +100,46 @@ def tile_attend_milweights_kernel(tc, inst_words, inst_scales, wv, wu, gain, sco
             return codes, scales
 
         ring = [psum.tile([P, BANK], F32, name="proj%d" % b) for b in range(PROJ_BANKS)]
-        turn = [0]
+        turns = []
 
         def project(weights, scale, low, width, result):
             codes, scales = weights
             half, at = divmod(low, HALF)
             per_bank = BANK // width
+            n = min(width, QUARTER)
             for first in range(0, PACK, per_bank):
-                bank = ring[turn[0] % PROJ_BANKS][:].rearrange("p (u i) -> p u i", u=per_bank)
-                turn.append(turn.pop() + 1)
+                bank = ring[len(turns) % PROJ_BANKS][:].rearrange("p (u i) -> p u i", u=per_bank)
+                turns.append(first)
                 for u in range(per_bank):
                     cols = slice((first + u) * P, (first + u + 1) * P)
-                    nc.tensor.matmul_mx(
-                        out=bank[:, u, :],
-                        lhsT=codes[:, cols].bitcast(FP8X4),
-                        lhsT_scale=scales[:, cols],
-                        rhs=inst_w[half][:, at : at + width].bitcast(FP8X4),
-                        rhs_scale=inst_s[:, low : low + width],
-                        start=True,
-                        stop=True,
-                    )
+                    for run in range(0, width, n):
+                        nc.tensor.matmul_mx(
+                            out=bank[:, u, run : run + n],
+                            lhsT=codes[:, cols].bitcast(FP8X4),
+                            lhsT_scale=scales[:, cols],
+                            rhs=inst_w[half][:, at + run : at + run + n].bitcast(FP8X4),
+                            rhs_scale=inst_s[:, low + run : low + run + n],
+                            start=True,
+                            stop=True,
+                        )
                 nc.scalar.activation(out=result[:, first : first + per_bank, :], in_=bank, func=ACT.Tanh, scale=scale)
 
-        def gate(tanh_half, result, scalar_tiles):
+        def gate(gate_tanh, result, scalar_tiles):
             for t in range(PACK):
                 factor = half_gains[:, t : t + 1]
                 if t < scalar_tiles:
                     nc.scalar.activation(
-                        out=result[:, t, :], in_=tanh_half[:, t, :], func=ACT.Identity, scale=factor, bias=factor
+                        out=result[:, t, :], in_=gate_tanh[:, t, :], func=ACT.Identity, scale=factor, bias=factor
                     )
                 else:
                     nc.vector.tensor_scalar(
                         out=result[:, t, :],
-                        in0=tanh_half[:, t, :],
+                        in0=gate_tanh[:, t, :],
                         scalar1=1.0,
                         scalar2=factor,
                         op0=ALU.add,
                         op1=ALU.mult,
                     )
-            return result
 
         starts = [sum(PIECES[:c]) for c in range(len(PIECES))]
 
@@ -142,35 +148,36 @@ def tile_attend_milweights_kernel(tc, inst_words, inst_scales, wv, wu, gain, sco
             project(wv_mx, 1.0, starts[c], PIECES[c], result)
             return result
 
-        inst_s = gather(pool_scales, U8, 0, SLOTS, "inst_s", "inst_s")
+        inst_s = gather(pool_scales, U8, 0, SLOTS, SLOTS, "inst_s", "inst_s")
         wu_mx = quantise_projection(wu_raw, (P // 2, P // 2), 1, "wu")
         inst_w = [
-            gather(pool_words, U32, 0, HALF, "first_words", "first_words"),
-            gather(pool_words, U32, HALF, SLOTS, "later_words", "wu_dealt"),
+            gather(pool_words, U32, 0, HALF, QUARTER, "first_words", "first_words"),
+            gather(pool_words, U32, HALF, SLOTS, HALF, "later_words", "wu_dealt"),
         ]
         wv_mx = quantise_projection(wv_raw, (WV_SCALAR_COLS, 0), 2, "wv")
-        tanh0 = shared[:, :, :HALF]
-        project(wu_mx, 0.5, 0, HALF, tanh0)
+
+        gate_tanh0 = shared[:, :, :HALF]
+        project(wu_mx, 0.5, 0, HALF, gate_tanh0)
         gate0 = keep.tile([P, PACK, HALF], F32, name="gate0", tag="wv_dealt", align_bytes=64)
 
-        score_packed = keep.tile([P, M, PACK], BF16, name="score_packed", align_bytes=64)[:]
+        score_packed = keep.tile([P, M, PACK], BF16, name="score_packed", align_bytes=64)
         score_codes = keep.tile([P, M], U32, name="score_codes", align_bytes=64)
         score_scales = keep.tile([P, M], U8, name="score_scales", align_bytes=64)
         nc.vector.tensor_copy(
-            out=score_packed.rearrange("p (c i) j -> p c j i", i=4),
-            in_=score_raw[:].rearrange("p j (c i) -> p c j i", i=4),
+            out=score_packed[:].rearrange("p (c i) j -> p c j i", i=RUN),
+            in_=score_raw[:].rearrange("p j (c i) -> p c j i", i=RUN),
         )
-        gates = [gate(tanh0, gate0[:], 0)]
+        gate(gate_tanh0, gate0[:], 0)
         nc.vector.quantize_mx(
             out=score_codes[:].bitcast(FP8X4),
             scales=score_scales[:],
-            in_=score_packed.rearrange("p m j -> p (m j)"),
+            in_=score_packed[:].rearrange("p m j -> p (m j)"),
         )
 
         def score_group(g):
             group = GROUPS[g]
-            total_width = sum(PIECES[c] for c in group)
-            x_packed = keep.tile([P, total_width, PACK], BF16, name="x_packed%d" % g, tag="x_packed%d" % g, align_bytes=64)
+            width = sum(PIECES[c] for c in group)
+            x_packed = keep.tile([P, width, PACK], BF16, name="x_packed%d" % g, align_bytes=64)
             for c in group:
                 half, at = divmod(starts[c], HALF)
                 low = starts[c] - starts[group[0]]
@@ -180,14 +187,14 @@ def tile_attend_milweights_kernel(tc, inst_words, inst_scales, wv, wu, gain, sco
                     in1=values[c][:].rearrange("p t (c i) -> p c t i", i=RUN),
                     op=ALU.mult,
                 )
-            x_codes = keep.tile([P, total_width], U32, name="x_codes%d" % g, align_bytes=64)
-            x_scales = keep.tile([P, total_width], U8, name="x_scales%d" % g, align_bytes=64)
+            x_codes = keep.tile([P, width], U32, name="x_codes%d" % g, align_bytes=64)
+            x_scales = keep.tile([P, width], U8, name="x_scales%d" % g, align_bytes=64)
             nc.vector.quantize_mx(
                 out=x_codes[:].bitcast(FP8X4),
                 scales=x_scales[:],
                 in_=x_packed[:].rearrange("p i t -> p (i t)"),
             )
-            logits = psum.tile([M, total_width], F32, name="logits%d" % g)
+            logits = psum.tile([M, width], F32, name="logits%d" % g)
             nc.tensor.matmul_mx(
                 out=logits[:],
                 lhsT=score_codes[:].bitcast(FP8X4),
@@ -218,10 +225,7 @@ def tile_attend_milweights_kernel(tc, inst_words, inst_scales, wv, wu, gain, sco
                     op=ALU.add,
                 )
                 nc.scalar.activation(out=p[:, :whole, :], in_=below[:], func=ACT.Exp)
-            return p, total
-
-        def exponentiate_bagwise(g, logits, minus_top, p, total):
-            for b in range(logits.shape[1] - BAGWISE_BAGS[g], logits.shape[1]):
+            for b in range(whole, bags):
                 nc.scalar.activation(
                     out=p[:, b, :],
                     in_=logits[:, b, :],
@@ -229,6 +233,7 @@ def tile_attend_milweights_kernel(tc, inst_words, inst_scales, wv, wu, gain, sco
                     bias=minus_top[:, b : b + 1],
                     accum_out=total[:, b : b + 1],
                 )
+            return p, total
 
         def invert(g, p, total):
             whole = p.shape[1] - BAGWISE_BAGS[g]
@@ -258,30 +263,28 @@ def tile_attend_milweights_kernel(tc, inst_words, inst_scales, wv, wu, gain, sco
                 )
 
         values = [value(0), value(1)]
-        tanh1 = keep.tile([P, PACK, HALF], F32, name="gate_tanh1")
+        gate_tanh1 = keep.tile([P, PACK, HALF], F32, name="gate_tanh1")
         gate1 = keep.tile([P, PACK, HALF], F32, name="gate1")
-        gates.append(gate1[:])
-        third = slice(0, PIECES[2])
-        last = slice(PIECES[2], HALF)
-        project(wu_mx, 0.5, HALF, PIECES[2], tanh1[:, :, third])
-        gate(tanh1[:, :, third], gate1[:, :, third], 0)
+        gates = [gate0, gate1]
+        third_quarter = slice(0, PIECES[2])
+        last_quarter = slice(PIECES[2], HALF)
+        project(wu_mx, 0.5, HALF, PIECES[2], gate_tanh1[:, :, third_quarter])
+        gate(gate_tanh1[:, :, third_quarter], gate1[:, :, third_quarter], 0)
         values.append(value(2))
-        project(wu_mx, 0.5, HALF + PIECES[2], HALF - PIECES[2], tanh1[:, :, last])
-        gate(tanh1[:, :, last], gate1[:, :, last], SCALAR_GATE_TILES)
+        project(wu_mx, 0.5, HALF + PIECES[2], HALF - PIECES[2], gate_tanh1[:, :, last_quarter])
+        gate(gate_tanh1[:, :, last_quarter], gate1[:, :, last_quarter], SCALAR_GATE_TILES)
         values.extend(value(c) for c in range(3, len(PIECES)))
+
         logits0 = score_group(0)
-        minus_top0 = maxima(0, logits0)
-        first = exponentiate(0, logits0, minus_top0)
-        exponentiate_bagwise(0, logits0, minus_top0, *first)
+        p0, total0 = exponentiate(0, logits0, maxima(0, logits0))
         logits1 = score_group(1)
         logits2 = score_group(2)
         minus_top1 = maxima(1, logits1)
-        inverse0 = invert(0, *first)
-        fourth = exponentiate(2, logits2, maxima(2, logits2))
-        second = exponentiate(1, logits1, minus_top1)
-        exponentiate_bagwise(1, logits1, minus_top1, *second)
-        normalise(0, first[0], inverse0, 1)
-        inverse2 = invert(2, *fourth)
-        inverse1 = invert(1, *second)
-        normalise(1, second[0], inverse1, 1)
-        normalise(2, fourth[0], inverse2, 2)
+        inverse0 = invert(0, p0, total0)
+        p2, total2 = exponentiate(2, logits2, maxima(2, logits2))
+        p1, total1 = exponentiate(1, logits1, minus_top1)
+        normalise(0, p0, inverse0, 1)
+        inverse2 = invert(2, p2, total2)
+        inverse1 = invert(1, p1, total1)
+        normalise(1, p1, inverse1, 1)
+        normalise(2, p2, inverse2, 2)

@@ -29,7 +29,7 @@ SPLIT = F // 2
 WV_SCALAR_COLS = 46
 SCALAR_GATE_TILES = 3
 SHARED_COLS = 128
-BAGWISE_BAGS = (8, 16, 6)
+BAGWISE_BAGS = (12, 16, 8)
 
 FLOPS = 2 * (2 * K * F * SLOTS + F * M * SLOTS)
 

@@ -25,6 +25,7 @@ PIECES = (256, 256, 256, 128, 128)
 GROUPS = ((0, 1), (2,), (3, 4))
 PROJ_BANKS = 5
 RUN = 4
+PRODUCT_RUN = 8
 SPLIT = F // 2
 WV_SCALAR_COLS = 46
 SCALAR_GATE_TILES = 3
@@ -52,8 +53,8 @@ def tile_attend_milweights_kernel(tc, inst_words, inst_scales, wv, wu, gain, sco
         wu_rows = wu.rearrange("(p j) f -> p j f", j=PACK)
         wv_rows = wv.rearrange("(p j) f -> p j f", j=PACK)
         word_rows = inst_words[0].rearrange("p n t -> p (n t)").bitcast(I32)
-        nc.sync.dma_start(offsets[:], offs)
         nc.sync.dma_start(out=wu_raw[0], in_=wu_rows[:, :, :SPLIT])
+        nc.sync.dma_start(offsets[:], offs)
         nc.vector.memset(pool_scales[:].bitcast(I32), 0)
         for r in range(4):
             nc.sync.dma_start(
@@ -182,9 +183,9 @@ def tile_attend_milweights_kernel(tc, inst_words, inst_scales, wv, wu, gain, sco
                 half, at = divmod(starts[c], HALF)
                 low = starts[c] - starts[group[0]]
                 nc.vector.tensor_tensor(
-                    out=x_packed[:, low : low + PIECES[c], :].rearrange("p (c i) t -> p c t i", i=RUN),
-                    in0=gates[half][:, :, at : at + PIECES[c]].rearrange("p t (c i) -> p c t i", i=RUN),
-                    in1=values[c][:].rearrange("p t (c i) -> p c t i", i=RUN),
+                    out=x_packed[:, low : low + PIECES[c], :].rearrange("p (c i) t -> p c t i", i=PRODUCT_RUN),
+                    in0=gates[half][:, :, at : at + PIECES[c]].rearrange("p t (c i) -> p c t i", i=PRODUCT_RUN),
+                    in1=values[c][:].rearrange("p t (c i) -> p c t i", i=PRODUCT_RUN),
                     op=ALU.mult,
                 )
             x_codes = keep.tile([P, width], U32, name="x_codes%d" % g, align_bytes=64)

@@ -226,7 +226,11 @@ def tile_attend_milweights_kernel(tc, inst_words, inst_scales, wv, wu, gain, sco
                     op=ALU.add,
                 )
                 nc.scalar.activation(out=p[:, :whole, :], in_=below[:], func=ACT.Exp)
-            for b in range(whole, bags):
+            return p, total
+
+        def bag_by_bag(g, logits, minus_top, p, total):
+            bags = logits.shape[1]
+            for b in range(bags - BAGWISE_BAGS[g], bags):
                 nc.scalar.activation(
                     out=p[:, b, :],
                     in_=logits[:, b, :],
@@ -234,34 +238,30 @@ def tile_attend_milweights_kernel(tc, inst_words, inst_scales, wv, wu, gain, sco
                     bias=minus_top[:, b : b + 1],
                     accum_out=total[:, b : b + 1],
                 )
-            return p, total
 
-        def invert(g, p, total):
+        def add_up(g, p, total):
             whole = p.shape[1] - BAGWISE_BAGS[g]
-            if whole > 0:
-                nc.vector.tensor_reduce(out=total[:, :whole], in_=p[:, :whole, :], axis=AXIS_X, op=ALU.add)
-            inverse = keep.tile([M, p.shape[1]], F32, name="inverse%d" % g)
-            nc.vector.reciprocal(out=inverse[:], in_=total[:])
+            nc.vector.tensor_reduce(out=total[:, :whole], in_=p[:, :whole, :], axis=AXIS_X, op=ALU.add)
+
+        def invert(total, name):
+            inverse = keep.tile([M, total.shape[1]], F32, name=name)
+            nc.vector.reciprocal(out=inverse[:], in_=total)
             return inverse
 
-        def normalise(g, p, inverse, parts):
-            bags = p.shape[1] // parts
-            weights = keep.tile([M, parts, bags, BAG], F32, name="weights%d" % g)
-            for part in range(parts):
-                some = slice(part * bags, (part + 1) * bags)
-                nc.vector.scalar_tensor_tensor(
-                    out=weights[:, part],
-                    in0=p[:, some, :],
-                    scalar=float(BAG),
-                    in1=inverse[:, some].unsqueeze(2).to_broadcast([M, bags, BAG]),
-                    op0=ALU.mult,
-                    op1=ALU.mult,
-                )
-                first_slot = starts[GROUPS[g][0]] + part * bags * BAG
-                nc.sync.dma_start(
-                    out=out[:, first_slot : first_slot + bags * BAG],
-                    in_=weights[:, part].rearrange("m g e -> m (g e)"),
-                )
+        def normalise(p, inverse, first_slot):
+            bags = p.shape[1]
+            weights = keep.tile([M, bags, BAG], F32, name="weights%d" % first_slot)
+            nc.vector.scalar_tensor_tensor(
+                out=weights[:],
+                in0=p,
+                scalar=float(BAG),
+                in1=inverse[:].unsqueeze(2).to_broadcast([M, bags, BAG]),
+                op0=ALU.mult,
+                op1=ALU.mult,
+            )
+            nc.sync.dma_start(
+                out=out[:, first_slot : first_slot + bags * BAG], in_=weights[:].rearrange("m g e -> m (g e)")
+            )
 
         values = [value(0), value(1)]
         gate_tanh1 = keep.tile([P, PACK, HALF], F32, name="gate_tanh1")
@@ -277,15 +277,23 @@ def tile_attend_milweights_kernel(tc, inst_words, inst_scales, wv, wu, gain, sco
         values.extend(value(c) for c in range(3, len(PIECES)))
 
         logits0 = score_group(0)
-        p0, total0 = exponentiate(0, logits0, maxima(0, logits0))
+        minus_top0 = maxima(0, logits0)
+        p0, total0 = exponentiate(0, logits0, minus_top0)
+        bag_by_bag(0, logits0, minus_top0, p0, total0)
         logits1 = score_group(1)
         logits2 = score_group(2)
         minus_top1 = maxima(1, logits1)
-        inverse0 = invert(0, p0, total0)
-        p2, total2 = exponentiate(2, logits2, maxima(2, logits2))
+        add_up(0, p0, total0)
+        inverse0 = invert(total0[:], "inverse0")
+        minus_top2 = maxima(2, logits2)
+        p2, total2 = exponentiate(2, logits2, minus_top2)
         p1, total1 = exponentiate(1, logits1, minus_top1)
-        normalise(0, p0, inverse0, 1)
-        inverse2 = invert(2, p2, total2)
-        inverse1 = invert(1, p1, total1)
-        normalise(1, p1, inverse1, 1)
-        normalise(2, p2, inverse2, 2)
+        bag_by_bag(1, logits1, minus_top1, p1, total1)
+        bag_by_bag(2, logits2, minus_top2, p2, total2)
+        normalise(p0[:], inverse0, 0)
+        inverse1 = invert(total1[:], "inverse1")
+        add_up(2, p2, total2)
+        normalise(p1[:], inverse1, HALF)
+        whole = p2.shape[1] - BAGWISE_BAGS[2]
+        normalise(p2[:, :whole], invert(total2[:, :whole], "inverse2"), HALF + QUARTER)
+        normalise(p2[:, whole:], invert(total2[:, whole:], "inverse3"), HALF + QUARTER + whole * BAG)

@@ -30,7 +30,7 @@ SPLIT = F // 2
 WV_SCALAR_COLS = 46
 SCALAR_GATE_TILES = 3
 SHARED_COLS = 128
-BAGWISE_BAGS = (12, 16, 8)
+BAGWISE_BAGS = (15, 16, 8)
 
 FLOPS = 2 * (2 * K * F * SLOTS + F * M * SLOTS)
 

@@ -62,9 +62,9 @@ def tile_attend_milweights_kernel(tc, inst_words, inst_scales, wv, wu, gain, sco
             )
         nc.sync.dma_start(out=wu_raw[1], in_=wu_rows[:, :, SPLIT:])
         nc.sync.dma_start(out=pool_words[:].bitcast(I32), in_=word_rows)
-        nc.sync.dma_start(out=gains[:], in_=gain.rearrange("(p t) o -> p (t o)", t=PACK))
         nc.sync.dma_start(out=wv_raw[0], in_=wv_rows[:, :, :SPLIT])
         nc.sync.dma_start(out=wv_raw[1], in_=wv_rows[:, :, SPLIT:])
+        nc.sync.dma_start(out=gains[:], in_=gain.rearrange("(p t) o -> p (t o)", t=PACK))
         nc.sync.dma_start(out=score_raw[:], in_=score.rearrange("(p j) m -> p j m", j=PACK))
 
         half_gains = keep.tile([P, PACK], F32, name="half_gains")

@@ -27,7 +27,7 @@ PROJ_BANKS = 5
 RUN = 4
 PRODUCT_RUN = 8
 SPLIT = F // 2
-WV_SCALAR_COLS = 46
+WV_SCALAR_COLS = 44
 SCALAR_GATE_TILES = 3
 SHARED_COLS = 128
 BAGWISE_BAGS = (15, 16, 8)
@@ -89,7 +89,13 @@ def tile_attend_milweights_kernel(tc, inst_words, inst_scales, wv, wu, gain, sco
                 if cols > 0:
                     nc.scalar.copy(out=part[:, :cols], in_=src[:, :cols])
                 if cols < P // 2:
-                    nc.vector.tensor_copy(out=part[:, cols:], in_=src[:, cols:])
+                    if cols > 0:
+                        nc.gpsimd.tensor_copy(
+                            out=part[:, cols:].rearrange("p q j t -> p t q j"),
+                            in_=src[:, cols:].rearrange("p q j t -> p t q j"),
+                        )
+                    else:
+                        nc.vector.tensor_copy(out=part, in_=src)
             flat = dealt[:].rearrange("p t q j -> p (t q j)")
             for low in range(0, F, F // calls):
                 high = low + F // calls

@@ -27,7 +27,8 @@ PROJ_BANKS = 5
 RUN = 4
 PRODUCT_RUN = 8
 SPLIT = F // 2
-WV_SCALAR_COLS = 44
+WV_SCALAR_COLS = 48
+WU_SCALAR_COLS = (56, 48)
 SCALAR_GATE_TILES = 3
 SHARED_COLS = 128
 BAGWISE_BAGS = (15, 16, 8)
@@ -156,7 +157,7 @@ def tile_attend_milweights_kernel(tc, inst_words, inst_scales, wv, wu, gain, sco
             return result
 
         inst_s = gather(pool_scales, U8, 0, SLOTS, SLOTS, "inst_s", "inst_s")
-        wu_mx = quantise_projection(wu_raw, (P // 2, P // 2), 1, "wu")
+        wu_mx = quantise_projection(wu_raw, WU_SCALAR_COLS, 1, "wu")
         inst_w = [
             gather(pool_words, U32, 0, HALF, QUARTER, "first_words", "first_words"),
             gather(pool_words, U32, HALF, SLOTS, HALF, "later_words", "wu_dealt"),

@@ -27,7 +27,7 @@ PROJ_BANKS = 5
 RUN = 4
 PRODUCT_RUN = 8
 SPLIT = F // 2
-WV_SCALAR_COLS = 48
+WV_SCALAR_COLS = 36
 WU_SCALAR_COLS = (56, 48)
 SCALAR_GATE_TILES = 3
 SHARED_COLS = 128
@@ -47,8 +47,13 @@ def tile_attend_milweights_kernel(tc, inst_words, inst_scales, wv, wu, gain, sco
         pool_words = keep.tile([P, T], U32, name="pool_words", align_bytes=64)
         gains = keep.tile([P, PACK], F32, name="gains")
         wu_raw = [keep.tile([P, PACK, SPLIT], F32, name="wu_raw%d" % h)[:] for h in range(2)]
-        shared = keep.tile([P, PACK, HALF + SPLIT - SHARED_COLS], F32, name="shared")
-        wv_raw = [shared[:, :, HALF - SHARED_COLS :], keep.tile([P, PACK, SPLIT], F32, name="wv_raw1")[:]]
+        raw_len = PACK * SPLIT
+        raw_end = 2 * HALF + QUARTER + SHARED_COLS
+        shared = keep.tile([P, PACK * HALF], F32, name="shared")
+        wv_raw = [
+            shared[:, raw_end - raw_len : raw_end].rearrange("p (j f) -> p j f", j=PACK),
+            keep.tile([P, PACK, SPLIT], F32, name="wv_raw1")[:],
+        ]
         score_raw = keep.tile([P, PACK, M], F32, name="score_raw")
 
         wu_rows = wu.rearrange("(p j) f -> p j f", j=PACK)
@@ -63,9 +68,9 @@ def tile_attend_milweights_kernel(tc, inst_words, inst_scales, wv, wu, gain, sco
             )
         nc.sync.dma_start(out=wu_raw[1], in_=wu_rows[:, :, SPLIT:])
         nc.sync.dma_start(out=pool_words[:].bitcast(I32), in_=word_rows)
+        nc.sync.dma_start(out=gains[:], in_=gain.rearrange("(p t) o -> p (t o)", t=PACK))
         nc.sync.dma_start(out=wv_raw[0], in_=wv_rows[:, :, :SPLIT])
         nc.sync.dma_start(out=wv_raw[1], in_=wv_rows[:, :, SPLIT:])
-        nc.sync.dma_start(out=gains[:], in_=gain.rearrange("(p t) o -> p (t o)", t=PACK))
         nc.sync.dma_start(out=score_raw[:], in_=score.rearrange("(p j) m -> p j m", j=PACK))
 
         half_gains = keep.tile([P, PACK], F32, name="half_gains")
@@ -73,7 +78,7 @@ def tile_attend_milweights_kernel(tc, inst_words, inst_scales, wv, wu, gain, sco
 
         def gather(pool, dtype, low, high, step, name, tag):
             picked = keep.tile([P, high - low], dtype, name=name, tag=tag, align_bytes=64)
-            for at in range(low, high, step):
+            for at in reversed(range(low, high, step)):
                 nc.vector.tensor_copy(
                     picked[:, at - low : at - low + step], pool[:].indirect(offsets[:, at // 16 : (at + step) // 16])
                 )
@@ -88,15 +93,16 @@ def tile_attend_milweights_kernel(tc, inst_words, inst_scales, wv, wu, gain, sco
                 src = raw[h].rearrange("p j (q t) -> p q j t", t=PACK)
                 part = dst[:, h * P // 2 : (h + 1) * P // 2]
                 if cols > 0:
-                    nc.scalar.copy(out=part[:, :cols], in_=src[:, :cols])
+                    nc.scalar.copy(out=part[:, P // 2 - cols :], in_=src[:, P // 2 - cols :])
                 if cols < P // 2:
                     if cols > 0:
                         nc.gpsimd.tensor_copy(
-                            out=part[:, cols:].rearrange("p q j t -> p t q j"),
-                            in_=src[:, cols:].rearrange("p q j t -> p t q j"),
+                            out=part[:, : P // 2 - cols].rearrange("p q j t -> p t q j"),
+                            in_=src[:, : P // 2 - cols].rearrange("p q j t -> p t q j"),
                         )
                     else:
-                        nc.vector.tensor_copy(out=part, in_=src)
+                        for pair in (slice(0, 2), slice(2, PACK)):
+                            nc.vector.tensor_copy(out=part[:, :, :, pair], in_=src[:, :, :, pair])
             flat = dealt[:].rearrange("p t q j -> p (t q j)")
             for low in range(0, F, F // calls):
                 high = low + F // calls
@@ -110,12 +116,12 @@ def tile_attend_milweights_kernel(tc, inst_words, inst_scales, wv, wu, gain, sco
         ring = [psum.tile([P, BANK], F32, name="proj%d" % b) for b in range(PROJ_BANKS)]
         turns = []
 
-        def project(weights, scale, low, width, result):
+        def project(weights, scale, low, width, result, firsts=None):
             codes, scales = weights
             half, at = divmod(low, HALF)
             per_bank = BANK // width
             n = min(width, QUARTER)
-            for first in range(0, PACK, per_bank):
+            for first in firsts or range(0, PACK, per_bank):
                 bank = ring[len(turns) % PROJ_BANKS][:].rearrange("p (u i) -> p u i", u=per_bank)
                 turns.append(first)
                 for u in range(per_bank):
@@ -164,8 +170,9 @@ def tile_attend_milweights_kernel(tc, inst_words, inst_scales, wv, wu, gain, sco
         ]
         wv_mx = quantise_projection(wv_raw, (WV_SCALAR_COLS, 0), 2, "wv")
 
-        gate_tanh0 = shared[:, :, :HALF]
-        project(wu_mx, 0.5, 0, HALF, gate_tanh0)
+        gate_tanh0 = shared[:].rearrange("p (t i) -> p t i", t=PACK)
+        project(wu_mx, 0.5, QUARTER, QUARTER, gate_tanh0[:, :, QUARTER:], (2, 0))
+        project(wu_mx, 0.5, 0, QUARTER, gate_tanh0[:, :, :QUARTER], (2, 0))
         gate0 = keep.tile([P, PACK, HALF], F32, name="gate0", tag="wv_dealt", align_bytes=64)
 
         score_packed = keep.tile([P, M, PACK], BF16, name="score_packed", align_bytes=64)

@@ -101,8 +101,7 @@ def tile_attend_milweights_kernel(tc, inst_words, inst_scales, wv, wu, gain, sco
                             in_=src[:, : P // 2 - cols].rearrange("p q j t -> p t q j"),
                         )
                     else:
-                        for pair in (slice(0, 2), slice(2, PACK)):
-                            nc.vector.tensor_copy(out=part[:, :, :, pair], in_=src[:, :, :, pair])
+                        nc.vector.tensor_copy(out=part, in_=src)
             flat = dealt[:].rearrange("p t q j -> p (t q j)")
             for low in range(0, F, F // calls):
                 high = low + F // calls

@@ -84,24 +84,27 @@ def tile_attend_milweights_kernel(tc, inst_words, inst_scales, wv, wu, gain, sco
                 )
             return picked
 
-        def quantise_projection(raw, scalar_cols, calls, name):
+        def quantise_projection(raw, shares, calls, name):
             dealt = keep.tile([P, PACK, P, PACK], BF16, name=name + "_dealt", tag=name + "_dealt", align_bytes=64)
             codes = keep.tile([P, F], U32, name=name + "_codes", align_bytes=64)
             scales = keep.tile([P, F], U8, name=name + "_scales", align_bytes=64)
             dst = dealt[:].rearrange("p t q j -> p q j t")
-            for h, cols in enumerate(scalar_cols):
+            for h, (pool_cols, scalar_cols, pairs) in enumerate(shares):
                 src = raw[h].rearrange("p j (q t) -> p q j t", t=PACK)
                 part = dst[:, h * P // 2 : (h + 1) * P // 2]
-                if cols > 0:
-                    nc.scalar.copy(out=part[:, P // 2 - cols :], in_=src[:, P // 2 - cols :])
-                if cols < P // 2:
-                    if cols > 0:
-                        nc.gpsimd.tensor_copy(
-                            out=part[:, : P // 2 - cols].rearrange("p q j t -> p t q j"),
-                            in_=src[:, : P // 2 - cols].rearrange("p q j t -> p t q j"),
+                last = P // 2 - scalar_cols
+                if scalar_cols > 0:
+                    nc.scalar.copy(out=part[:, last:], in_=src[:, last:])
+                if pool_cols > 0:
+                    nc.gpsimd.tensor_copy(
+                        out=part[:, :pool_cols].rearrange("p q j t -> p t q j"),
+                        in_=src[:, :pool_cols].rearrange("p q j t -> p t q j"),
+                    )
+                if pool_cols < last:
+                    for pair in pairs:
+                        nc.vector.tensor_copy(
+                            out=part[:, pool_cols:last, :, pair], in_=src[:, pool_cols:last, :, pair]
                         )
-                    else:
-                        nc.vector.tensor_copy(out=part, in_=src)
             flat = dealt[:].rearrange("p t q j -> p (t q j)")
             for low in range(0, F, F // calls):
                 high = low + F // calls
@@ -162,12 +165,14 @@ def tile_attend_milweights_kernel(tc, inst_words, inst_scales, wv, wu, gain, sco
             return result
 
         inst_s = gather(pool_scales, U8, 0, SLOTS, SLOTS, "inst_s", "inst_s")
-        wu_mx = quantise_projection(wu_raw, WU_SCALAR_COLS, 1, "wu")
+        wu_mx = quantise_projection(wu_raw, [(8, 56, ()), (16, 48, ())], 1, "wu")
         inst_w = [
             gather(pool_words, U32, 0, HALF, QUARTER, "first_words", "first_words"),
             gather(pool_words, U32, HALF, SLOTS, HALF, "later_words", "wu_dealt"),
         ]
-        wv_mx = quantise_projection(wv_raw, (WV_SCALAR_COLS, 0), 2, "wv")
+        wv_mx = quantise_projection(
+            wv_raw, [(28, 36, ()), (0, 12, [slice(0, PACK)])], 2, "wv"
+        )
 
         gate_tanh0 = shared[:].rearrange("p (t i) -> p t i", t=PACK)
         project(wu_mx, 0.5, QUARTER, QUARTER, gate_tanh0[:, :, QUARTER:], (2, 0))

@@ -97,8 +97,8 @@ def tile_attend_milweights_kernel(tc, inst_words, inst_scales, wv, wu, gain, sco
                     nc.scalar.copy(out=part[:, last:], in_=src[:, last:])
                 if pool_cols > 0:
                     nc.gpsimd.tensor_copy(
-                        out=part[:, :pool_cols].rearrange("p q j t -> p t q j"),
-                        in_=src[:, :pool_cols].rearrange("p q j t -> p t q j"),
+                        out=part[:, :pool_cols].rearrange("p q j t -> p q t j"),
+                        in_=src[:, :pool_cols].rearrange("p q j t -> p q t j"),
                     )
                 if pool_cols < last:
                     for pair in pairs:

from contextlib import ExitStack

import concourse.mybir as mybir

F32 = mybir.dt.float32
BF16 = mybir.dt.bfloat16
I32 = mybir.dt.int32
U32 = mybir.dt.uint32
U16 = mybir.dt.uint16
U8 = mybir.dt.uint8
FP8X4 = mybir.dt.float8_e4m3fn_x4
ALU = mybir.AluOpType
ACT = mybir.ActivationFunctionType
AXIS_X = mybir.AxisListType.X

P = 128
PACK = 4
K, T, SLOTS, F, M = 512, 2048, 1024, 512, 128
BAG = 16
BANK = 512
HALF = SLOTS // 2
QUARTER = SLOTS // 4

PIECES = (256, 256, 256, 128, 128)
GROUPS = ((0, 1), (2,), (3, 4))
PROJ_BANKS = 5
RUN = 4
PRODUCT_RUN = 8
SPLIT = F // 2
WV_SCALAR_COLS = 36
WU_SCALAR_COLS = (56, 48)
SCALAR_GATE_TILES = 3
SHARED_COLS = 128
BAGWISE_BAGS = (15, 16, 8)

FLOPS = 2 * (2 * K * F * SLOTS + F * M * SLOTS)


def tile_attend_milweights_kernel(tc, inst_words, inst_scales, wv, wu, gain, score, offs, out):
    nc = tc.nc
    with ExitStack() as ctx:
        keep = ctx.enter_context(tc.tile_pool(name="keep", bufs=1))
        psum = ctx.enter_context(tc.psum_pool(name="psum", bufs=1))

        offsets = keep.tile([P, SLOTS // 16], U16, name="offsets")
        pool_scales = keep.tile([P, T], U8, name="pool_scales", align_bytes=64)
        pool_words = keep.tile([P, T], U32, name="pool_words", align_bytes=64)
        gains = keep.tile([P, PACK], F32, name="gains")
        wu_raw = [keep.tile([P, PACK, SPLIT], F32, name="wu_raw%d" % h)[:] for h in range(2)]
        raw_len = PACK * SPLIT
        raw_end = 2 * HALF + QUARTER + SHARED_COLS
        shared = keep.tile([P, PACK * HALF], F32, name="shared")
        wv_raw = [
            shared[:, raw_end - raw_len : raw_end].rearrange("p (j f) -> p j f", j=PACK),
            keep.tile([P, PACK, SPLIT], F32, name="wv_raw1")[:],
        ]
        score_raw = keep.tile([P, PACK, M], F32, name="score_raw")

        wu_rows = wu.rearrange("(p j) f -> p j f", j=PACK)
        wv_rows = wv.rearrange("(p j) f -> p j f", j=PACK)
        word_rows = inst_words[0].rearrange("p n t -> p (n t)").bitcast(I32)
        nc.sync.dma_start(out=wu_raw[0], in_=wu_rows[:, :, :SPLIT])
        nc.sync.dma_start(offsets[:], offs)
        nc.vector.memset(pool_scales[:].bitcast(I32), 0)
        for r in range(4):
            nc.sync.dma_start(
                out=pool_scales[r:P:32, :].bitcast(I32), in_=inst_scales[0, r:16:4, :].bitcast(I32)
            )
        nc.sync.dma_start(out=wu_raw[1], in_=wu_rows[:, :, SPLIT:])
        nc.sync.dma_start(out=pool_words[:].bitcast(I32), in_=word_rows)
        nc.sync.dma_start(out=gains[:], in_=gain.rearrange("(p t) o -> p (t o)", t=PACK))
        nc.sync.dma_start(out=wv_raw[0], in_=wv_rows[:, :, :SPLIT])
        nc.sync.dma_start(out=wv_raw[1], in_=wv_rows[:, :, SPLIT:])
        nc.sync.dma_start(out=score_raw[:], in_=score.rearrange("(p j) m -> p j m", j=PACK))

        half_gains = keep.tile([P, PACK], F32, name="half_gains")
        nc.scalar.activation(out=half_gains[:], in_=gains[:], func=ACT.Copy, scale=0.5)

        def gather(pool, dtype, low, high, step, name, tag):
            picked = keep.tile([P, high - low], dtype, name=name, tag=tag, align_bytes=64)
            for at in reversed(range(low, high, step)):
                nc.vector.tensor_copy(
                    picked[:, at - low : at - low + step], pool[:].indirect(offsets[:, at // 16 : (at + step) // 16])
                )
            return picked

        def quantise_projection(raw, shares, calls, name):
            dealt = keep.tile([P, PACK, P, PACK], BF16, name=name + "_dealt", tag=name + "_dealt", align_bytes=64)
            codes = keep.tile([P, F], U32, name=name + "_codes", align_bytes=64)
            scales = keep.tile([P, F], U8, name=name + "_scales", align_bytes=64)
            dst = dealt[:].rearrange("p t q j -> p q j t")
            for h, (pool_cols, scalar_cols, pairs) in enumerate(shares):
                src = raw[h].rearrange("p j (q t) -> p q j t", t=PACK)
                part = dst[:, h * P // 2 : (h + 1) * P // 2]
                last = P // 2 - scalar_cols
                if scalar_cols > 0:
                    nc.scalar.copy(out=part[:, last:], in_=src[:, last:])
                if pool_cols > 0:
                    nc.gpsimd.tensor_copy(
                        out=part[:, :pool_cols].rearrange("p q j t -> p q t j"),
                        in_=src[:, :pool_cols].rearrange("p q j t -> p q t j"),
                    )
                if pool_cols < last:
                    for pair in pairs:
                        nc.vector.tensor_copy(
                            out=part[:, pool_cols:last, :, pair], in_=src[:, pool_cols:last, :, pair]
                        )
            flat = dealt[:].rearrange("p t q j -> p (t q j)")
            for low in range(0, F, F // calls):
                high = low + F // calls
                nc.vector.quantize_mx(
                    out=codes[:, low:high].bitcast(FP8X4),
                    scales=scales[:, low:high],
                    in_=flat[:, low * PACK : high * PACK],
                )
            return codes, scales

        ring = [psum.tile([P, BANK], F32, name="proj%d" % b) for b in range(PROJ_BANKS)]
        turns = []

        def project(weights, scale, low, width, result, firsts=None):
            codes, scales = weights
            half, at = divmod(low, HALF)
            per_bank = BANK // width
            n = min(width, QUARTER)
            for first in firsts or range(0, PACK, per_bank):
                bank = ring[len(turns) % PROJ_BANKS][:].rearrange("p (u i) -> p u i", u=per_bank)
                turns.append(first)
                for u in range(per_bank):
                    cols = slice((first + u) * P, (first + u + 1) * P)
                    for run in range(0, width, n):
                        nc.tensor.matmul_mx(
                            out=bank[:, u, run : run + n],
                            lhsT=codes[:, cols].bitcast(FP8X4),
                            lhsT_scale=scales[:, cols],
                            rhs=inst_w[half][:, at + run : at + run + n].bitcast(FP8X4),
                            rhs_scale=inst_s[:, low + run : low + run + n],
                            start=True,
                            stop=True,
                        )
                nc.scalar.activation(out=result[:, first : first + per_bank, :], in_=bank, func=ACT.Tanh, scale=scale)

        def gate(gate_tanh, result, scalar_tiles):
            for t in range(PACK):
                factor = half_gains[:, t : t + 1]
                if t < scalar_tiles:
                    nc.scalar.activation(
                        out=result[:, t, :], in_=gate_tanh[:, t, :], func=ACT.Identity, scale=factor, bias=factor
                    )
                else:
                    nc.vector.tensor_scalar(
                        out=result[:, t, :],
                        in0=gate_tanh[:, t, :],
                        scalar1=1.0,
                        scalar2=factor,
                        op0=ALU.add,
                        op1=ALU.mult,
                    )

        starts = [sum(PIECES[:c]) for c in range(len(PIECES))]

        def value(c):
            result = keep.tile([P, PACK, PIECES[c]], F32, name="value%d" % c)
            project(wv_mx, 1.0, starts[c], PIECES[c], result)
            return result

        inst_s = gather(pool_scales, U8, 0, SLOTS, SLOTS, "inst_s", "inst_s")
        wu_mx = quantise_projection(wu_raw, [(8, 56, ()), (16, 48, ())], 1, "wu")
        inst_w = [
            gather(pool_words, U32, 0, HALF, QUARTER, "first_words", "first_words"),
            gather(pool_words, U32, HALF, SLOTS, HALF, "later_words", "wu_dealt"),
        ]
        wv_mx = quantise_projection(
            wv_raw, [(28, 36, ()), (0, 12, [slice(0, PACK)])], 2, "wv"
        )

        gate_tanh0 = shared[:].rearrange("p (t i) -> p t i", t=PACK)
        project(wu_mx, 0.5, QUARTER, QUARTER, gate_tanh0[:, :, QUARTER:], (2, 0))
        project(wu_mx, 0.5, 0, QUARTER, gate_tanh0[:, :, :QUARTER], (2, 0))
        gate0 = keep.tile([P, PACK, HALF], F32, name="gate0", tag="wv_dealt", align_bytes=64)

        score_packed = keep.tile([P, M, PACK], BF16, name="score_packed", align_bytes=64)
        score_codes = keep.tile([P, M], U32, name="score_codes", align_bytes=64)
        score_scales = keep.tile([P, M], U8, name="score_scales", align_bytes=64)
        nc.vector.tensor_copy(
            out=score_packed[:].rearrange("p (c i) j -> p c j i", i=RUN),
            in_=score_raw[:].rearrange("p j (c i) -> p c j i", i=RUN),
        )
        gate(gate_tanh0, gate0[:], 0)
        nc.vector.quantize_mx(
            out=score_codes[:].bitcast(FP8X4),
            scales=score_scales[:],
            in_=score_packed[:].rearrange("p m j -> p (m j)"),
        )

        def score_group(g):
            group = GROUPS[g]
            width = sum(PIECES[c] for c in group)
            x_packed = keep.tile([P, width, PACK], BF16, name="x_packed%d" % g, align_bytes=64)
            for c in group:
                half, at = divmod(starts[c], HALF)
                low = starts[c] - starts[group[0]]
                nc.vector.tensor_tensor(
                    out=x_packed[:, low : low + PIECES[c], :].rearrange("p (c i) t -> p c t i", i=PRODUCT_RUN),
                    in0=gates[half][:, :, at : at + PIECES[c]].rearrange("p t (c i) -> p c t i", i=PRODUCT_RUN),
                    in1=values[c][:].rearrange("p t (c i) -> p c t i", i=PRODUCT_RUN),
                    op=ALU.mult,
                )
            x_codes = keep.tile([P, width], U32, name="x_codes%d" % g, align_bytes=64)
            x_scales = keep.tile([P, width], U8, name="x_scales%d" % g, align_bytes=64)
            nc.vector.quantize_mx(
                out=x_codes[:].bitcast(FP8X4),
                scales=x_scales[:],
                in_=x_packed[:].rearrange("p i t -> p (i t)"),
            )
            logits = psum.tile([M, width], F32, name="logits%d" % g)
            nc.tensor.matmul_mx(
                out=logits[:],
                lhsT=score_codes[:].bitcast(FP8X4),
                lhsT_scale=score_scales[:],
                rhs=x_codes[:].bitcast(FP8X4),
                rhs_scale=x_scales[:],
                start=True,
                stop=True,
            )
            return logits[:].rearrange("m (g e) -> m g e", e=BAG)

        def maxima(g, logits):
            minus_top = keep.tile([M, logits.shape[1]], F32, name="minus_top%d" % g)
            nc.vector.tensor_reduce(out=minus_top[:], in_=logits, axis=AXIS_X, op=ALU.max, negate=True)
            return minus_top

        def exponentiate(g, logits, minus_top):
            bags = logits.shape[1]
            p = keep.tile([M, bags, BAG], F32, name="p%d" % g)
            total = keep.tile([M, bags], F32, name="total%d" % g)
            whole = bags - BAGWISE_BAGS[g]
            if whole > 0:
                below = keep.tile([M, whole, BAG], F32, name="below%d" % g)
                nc.vector.tensor_tensor(
                    out=below[:],
                    in0=logits[:, :whole, :],
                    in1=minus_top[:, :whole].unsqueeze(2).to_broadcast([M, whole, BAG]),
                    op=ALU.add,
                )
                nc.scalar.activation(out=p[:, :whole, :], in_=below[:], func=ACT.Exp)
            return p, total

        def bag_by_bag(g, logits, minus_top, p, total):
            bags = logits.shape[1]
            for b in range(bags - BAGWISE_BAGS[g], bags):
                nc.scalar.activation(
                    out=p[:, b, :],
                    in_=logits[:, b, :],
                    func=ACT.Exp,
                    bias=minus_top[:, b : b + 1],
                    accum_out=total[:, b : b + 1],
                )

        def add_up(g, p, total):
            whole = p.shape[1] - BAGWISE_BAGS[g]
            nc.vector.tensor_reduce(out=total[:, :whole], in_=p[:, :whole, :], axis=AXIS_X, op=ALU.add)

        def invert(total, name):
            inverse = keep.tile([M, total.shape[1]], F32, name=name)
            nc.vector.reciprocal(out=inverse[:], in_=total)
            return inverse

        def normalise(p, inverse, first_slot):
            bags = p.shape[1]
            weights = keep.tile([M, bags, BAG], F32, name="weights%d" % first_slot)
            nc.vector.scalar_tensor_tensor(
                out=weights[:],
                in0=p,
                scalar=float(BAG),
                in1=inverse[:].unsqueeze(2).to_broadcast([M, bags, BAG]),
                op0=ALU.mult,
                op1=ALU.mult,
            )
            nc.sync.dma_start(
                out=out[:, first_slot : first_slot + bags * BAG], in_=weights[:].rearrange("m g e -> m (g e)")
            )

        values = [value(0), value(1)]
        gate_tanh1 = keep.tile([P, PACK, HALF], F32, name="gate_tanh1")
        gate1 = keep.tile([P, PACK, HALF], F32, name="gate1")
        gates = [gate0, gate1]
        third_quarter = slice(0, PIECES[2])
        last_quarter = slice(PIECES[2], HALF)
        project(wu_mx, 0.5, HALF, PIECES[2], gate_tanh1[:, :, third_quarter])
        gate(gate_tanh1[:, :, third_quarter], gate1[:, :, third_quarter], 0)
        values.append(value(2))
        project(wu_mx, 0.5, HALF + PIECES[2], HALF - PIECES[2], gate_tanh1[:, :, last_quarter])
        gate(gate_tanh1[:, :, last_quarter], gate1[:, :, last_quarter], SCALAR_GATE_TILES)
        values.extend(value(c) for c in range(3, len(PIECES)))

        logits0 = score_group(0)
        minus_top0 = maxima(0, logits0)
        p0, total0 = exponentiate(0, logits0, minus_top0)
        bag_by_bag(0, logits0, minus_top0, p0, total0)
        logits1 = score_group(1)
        logits2 = score_group(2)
        minus_top1 = maxima(1, logits1)
        add_up(0, p0, total0)
        inverse0 = invert(total0[:], "inverse0")
        minus_top2 = maxima(2, logits2)
        p2, total2 = exponentiate(2, logits2, minus_top2)
        p1, total1 = exponentiate(1, logits1, minus_top1)
        bag_by_bag(1, logits1, minus_top1, p1, total1)
        bag_by_bag(2, logits2, minus_top2, p2, total2)
        normalise(p0[:], inverse0, 0)
        inverse1 = invert(total1[:], "inverse1")
        add_up(2, p2, total2)
        normalise(p1[:], inverse1, HALF)
        whole = p2.shape[1] - BAGWISE_BAGS[2]
        normalise(p2[:, :whole], invert(total2[:, :whole], "inverse2"), HALF + QUARTER)
        normalise(p2[:, whole:], invert(total2[:, whole:], "inverse3"), HALF + QUARTER + whole * BAG)
